import numpy as np
import ml_dtypes


def mxq(x, axis, fmt="e4m3"):
    dtype, down = {"e4m3": (ml_dtypes.float8_e4m3fn, 7), "e5m2": (ml_dtypes.float8_e5m2, 14)}[fmt]
    v = np.moveaxis(np.asarray(x, np.float32).astype(ml_dtypes.bfloat16).astype(np.float64), axis, -1)
    blocks = v.reshape(v.shape[:-1] + (-1, 32))
    amax = np.abs(blocks).max(-1, keepdims=True)
    byte = np.maximum(np.where(amax > 0, np.frexp(amax)[1] - 1 + 127, 0) - down, 1)
    scale = np.exp2(byte - 127.0)
    codes = (blocks / scale).astype(np.float32).astype(dtype).astype(np.float64)
    return np.moveaxis((codes * scale).reshape(v.shape), -1, axis)


WIDE = False


def mx_kscale(k):
    if not WIDE:
        return np.ones(k)
    levels = np.array([10, -10, 5, -5, 0])
    if k % 512:
        return np.exp2(np.random.permutation(np.resize(levels, k // 32))).repeat(32)
    a = np.empty((k // 512, 16))
    for p in range(k // 512):
        a[p, :8] = np.random.permutation(np.resize(levels, 8))
        for g in range(8):
            far = levels[np.abs(levels - a[p, g]) >= 10]
            a[p, g + 8] = far[np.random.randint(len(far))]
    return np.exp2(a.ravel()).repeat(32)


BF16 = ml_dtypes.bfloat16


def bf(x):
    return np.asarray(x, np.float32).astype(BF16)


def f64(x):
    return np.asarray(x).astype(np.float64)


E2M1 = np.array([0.0, 0.5, 1.0, 1.5, 2.0, 3.0, 4.0, 6.0, -0.0, -0.5, -1.0, -1.5, -2.0, -3.0, -4.0, -6.0])


def pack_weight(w, fmt):
    k, n = w.shape
    w = f64(bf(w)).reshape(k // 32, 32, n)
    amax = np.abs(w).max(1)
    if fmt == "e4m3":
        byte = np.frexp(amax)[1] - 1 + 127 - 7
    else:
        mant, ex = np.frexp(amax / 6.0)
        byte = np.where(mant > 0.5, ex, ex - 1) + 127
    byte = np.clip(np.where(amax > 0, byte, 1), 1, 254)
    scaled = (w * np.exp2(127.0 - byte)[:, None, :]).reshape(k, n).astype(np.float32)
    by_word = np.ascontiguousarray(scaled.reshape(k // 512, 128, 4, n).transpose(0, 1, 3, 2))
    if fmt == "e4m3":
        words = by_word.astype(ml_dtypes.float8_e4m3fn).view(np.uint8)
    else:
        c = by_word.astype(ml_dtypes.float4_e2m1fn).view(np.uint8) & 0xF
        words = c[..., 0::2] | (c[..., 1::2] << 4)
    return np.ascontiguousarray(words), np.ascontiguousarray(byte.astype(np.uint8).reshape(k // 512, 16, n))


def unpack_weight(words, scales, fmt):
    g, p, n, _ = words.shape
    if fmt == "e4m3":
        vals = np.ascontiguousarray(words).view(ml_dtypes.float8_e4m3fn).astype(np.float64)
    else:
        nib = np.empty((g, p, n, 4), np.uint8)
        nib[..., 0::2] = words & 0xF
        nib[..., 1::2] = words >> 4
        vals = E2M1[nib]
    vals = vals * np.repeat(np.exp2(scales.astype(np.float64) - 127.0), 8, axis=1)[..., None]
    return vals.transpose(0, 1, 3, 2).reshape(g * 512, n)
def pack4(w):
    words, scales = pack_weight(w, "e2m1")
    return words.reshape(words.shape[0], 128, -1), scales


def unpack4(words, scales):
    return unpack_weight(words.reshape(words.shape[0], 128, -1, 2), scales, "e2m1")


E4M3FN = np.array([(-1.0 if i & 128 else 1.0) * ((1.0 + (i & 7) / 8.0) * 2.0 ** (((i >> 3) & 15) - 7) if i & 120 else (i & 7) * 2.0 ** -9) for i in range(256)])


def e4m3fn_bytes(y):
    return np.clip(np.asarray(y, np.float64), -448.0, 448.0).astype(np.float32).astype(ml_dtypes.float8_e4m3fn).view(np.uint8)


def e4m3fn_values(b):
    return E4M3FN[b]

def planes(Y):
    n, m = Y.shape
    b = f64(bf(Y)).reshape(n // 32, 32, m)
    amax = np.abs(b).max(1)
    byte = np.clip(np.where(amax > 0, np.frexp(amax)[1] - 1 + 127 - 7, 1), 1, 254)
    codes = (b * np.exp2(127.0 - byte)[:, None, :]).reshape(n, m).astype(np.float32).astype(ml_dtypes.float8_e4m3fn).view(np.uint8)
    words = codes.reshape(n // 512, 128, 4, m).transpose(0, 1, 3, 2)
    return np.ascontiguousarray(words), np.ascontiguousarray(byte.astype(np.uint8).reshape(n // 512, 16, m))


S, R, H, D, B = 2048, 1024, 8, 128, 128
F = H * D
FMAX = 448.0


def setup_inputs():
    s = mx_kscale(R)
    C = np.random.randn(S, R) * np.exp(0.7 * np.random.randn(S, 1)) * s[None, :]
    C_scale = (np.abs(C).reshape(S, R // B, B).max(axis=2) / FMAX).astype(np.float32)
    C_bytes = e4m3fn_bytes(C / np.repeat(f64(C_scale), B, axis=1))
    Wk = np.random.randn(R, F) / np.sqrt(R) / s[:, None]
    Wv = np.random.randn(R, F) / np.sqrt(R) / s[:, None]
    k_words, k_scales = pack4(Wk)
    v_words, v_scales = pack4(Wv)
    return {
        "C_bytes": C_bytes,
        "C_scale": C_scale,
        "k_words": k_words,
        "k_scales": k_scales,
        "v_words": v_words,
        "v_scales": v_scales,
        "k_bias": bf(0.5 * np.random.randn(1, F)),
        "v_bias": bf(0.5 * np.random.randn(1, F)),
    }


def reference(C_bytes, C_scale, k_words, k_scales, v_words, v_scales, k_bias, v_bias):
    C = e4m3fn_values(C_bytes) * np.repeat(f64(C_scale), B, axis=1)
    c = mxq(C, 1, "e4m3")
    key = (c @ unpack4(k_words, k_scales)) + f64(k_bias)
    value = (c @ unpack4(v_words, v_scales)) + f64(v_bias)
    y = np.stack([key, value], axis=1).reshape(S, -1, H, D)
    Y = y.reshape(S, -1)
    words, scales = planes(Y)
    return y, words, scales

@@ -1,0 +1,358 @@
+from contextlib import ExitStack
+
+import concourse.mybir as mybir
+from concourse.masks import make_identity
+
+F32 = mybir.dt.float32
+BF16 = mybir.dt.bfloat16
+I32 = mybir.dt.int32
+U32 = mybir.dt.uint32
+U8 = mybir.dt.uint8
+FP8 = mybir.dt.float8_e4m3fn
+FP8X4 = mybir.dt.float8_e4m3fn_x4
+FP4X4 = mybir.dt.float4_e2m1fn_x4
+ADD = mybir.AluOpType.add
+MULT = mybir.AluOpType.mult
+COPY = mybir.ActivationFunctionType.Copy
+
+S, R, F = 2048, 1024, 1024
+P = 128
+PACK = 4
+GROUP = P * PACK
+GROUPS = S // GROUP
+SLOTS = GROUPS * PACK
+PASSES = R // GROUP
+BLOCK = 128
+BLOCKS = R // BLOCK
+N = 512
+CHUNKS = F // N
+HALVES = 2 * GROUPS
+RUN = 4
+
+FLOPS = 2 * S * R * 2 * F
+
+
+def tile_latent_cache_key_value_b2_kernel(
+    tc, C_bytes, C_scale, k_words, k_scales, v_words, v_scales, k_bias, v_bias, out_0, out_1, out_2
+):
+    nc = tc.nc
+    c_rows = C_bytes.rearrange("(g p t) k -> g p (t k)", p=P, t=PACK)
+    c_scale_rows = C_scale.rearrange("(g p t) b -> p g (t b)", p=P, t=PACK)
+    y_rows = out_0.rearrange("(g p t) j h d -> g j p t (h d)", p=P, t=PACK)
+    y_words = out_1.rearrange("g p m t -> g p (m t)").bitcast(I32)
+    y_scales = out_2.bitcast(I32)
+
+    with ExitStack() as ctx:
+        keep = ctx.enter_context(tc.tile_pool(name="keep", bufs=1))
+        flow = ctx.enter_context(tc.tile_pool(name="flow", bufs=2))
+        psum = ctx.enter_context(tc.psum_pool(name="psum", bufs=2))
+        ctx.enter_context(tc.manual_schedule())
+
+        ident = keep.tile([P, P], F32, name="ident")
+        make_identity(nc, ident[:])
+        bias = keep.tile([P, 2 * F], BF16, name="bias")
+        w_words, w_scales, bias_words = [], [], []
+        for j in range(2):
+            w_words.append(keep.tile([P, PASSES, 2 * F], U8, name="w_words%d" % j, align_bytes=64))
+            w_scales.append(keep.tile([P, PASSES, F], U8, name="w_scales%d" % j, align_bytes=64))
+            bias_words.append(keep.tile([P, F // P], BF16, name="bias_words%d" % j))
+            nc.vector.memset(w_scales[j][:].rearrange("p g n -> p (g n)").bitcast(I32), 0)
+
+        raw, row_scale = {}, {}
+
+        def load_bytes(g, t0, t1):
+            tile = keep.tile([P, (t1 - t0) * R], U8, name="raw%d_%d" % (g, t0))
+            nc.sync.dma_start(out=tile[:], in_=c_rows[g][:, t0 * R : t1 * R])
+            for t in range(t0, t1):
+                raw[PACK * g + t] = tile[:, (t - t0) * R : (t - t0 + 1) * R]
+
+        def load_row_scales(queue, g0, g1):
+            tile = keep.tile([P, g1 - g0, PACK * BLOCKS], F32, name="row_scale%d" % g0)
+            queue.dma_start(out=tile[:], in_=c_scale_rows[:, g0:g1, :])
+            for g in range(g0, g1):
+                for t in range(PACK):
+                    row_scale[PACK * g + t] = tile[:, g - g0, t * BLOCKS : (t + 1) * BLOCKS]
+
+        def load_w_words(j):
+            words = (k_words, v_words)[j]
+            nc.sync.dma_start(
+                out=w_words[j][:].bitcast(I32), in_=words.rearrange("g p n -> p g n").bitcast(I32)
+            )
+
+        def load_w_scales(j):
+            scales = (k_scales, v_scales)[j]
+            for q in range(4):
+                nc.sync.dma_start(
+                    out=w_scales[j][32 * q : 32 * q + 4, :, :].bitcast(I32),
+                    in_=scales[:, 4 * q : 4 * q + 4, :].rearrange("g r n -> r g n").bitcast(I32),
+                )
+
+        def load_bias(j):
+            row = (k_bias, v_bias)[j]
+            nc.sync.dma_start(out=bias_words[j][:], in_=row.rearrange("o (p e) -> p (o e)", p=P))
+
+        load_row_scales(nc.scalar, 0, 1)
+        load_bytes(0, 0, 1)
+        load_w_scales(0)
+        load_bytes(0, 1, PACK)
+        load_w_words(0)
+        load_bias(0)
+        load_bytes(1, 0, PACK)
+        load_row_scales(nc.sync, 1, GROUPS)
+        load_w_scales(1)
+        load_bias(1)
+        load_w_words(1)
+        for g in range(2, GROUPS):
+            load_bytes(g, 0, PACK)
+
+        wide, turned, grouped, c_codes, c_planes = {}, {}, {}, {}, {}
+        y_f32, y_bf16, y_codes, y_planes = {}, {}, {}, {}
+
+        def spread_bias(j):
+            bank = psum.tile([P, PACK, P], F32, tag="turn", name="bias_bank")
+            words = bias_words[j][:].bitcast(F32)
+            for e in range(PACK):
+                nc.tensor.transpose(bank[:, e, :], words[:, e : e + 1].to_broadcast([P, P]), ident[:])
+            nc.scalar.copy(
+                out=bias[:, j * F : (j + 1) * F].bitcast(F32).rearrange("p (n e) -> p n e", e=PACK),
+                in_=bank[:].rearrange("p e n -> p n e"),
+            )
+
+        def widen_on_vector(s):
+            wide[s] = flow.tile([P, R], BF16, tag="wide", name="wide", bufs=4)
+            sorted_view = wide[s][:].rearrange("p (g u q e) -> p g q u e", g=PASSES, u=2, e=2)
+            for b in range(BLOCKS):
+                g, q0 = b // PACK, 32 * (b % PACK)
+                nc.vector.tensor_scalar(
+                    out=sorted_view[:, g, q0 : q0 + 32, :, :],
+                    in0=raw[s][:, b * BLOCK : (b + 1) * BLOCK].bitcast(FP8).rearrange("p (q u e) -> p q u e", u=2, e=2),
+                    scalar1=row_scale[s][:, b : b + 1],
+                    scalar2=None,
+                    op0=MULT,
+                )
+
+        def widen_on_scalar(s):
+            wide[s] = flow.tile([P, R], BF16, tag="wide", name="wide", bufs=4)
+            for b in range(BLOCKS):
+                cols = slice(b * BLOCK, (b + 1) * BLOCK)
+                nc.scalar.activation(
+                    out=wide[s][:, cols], in_=raw[s][:, cols].bitcast(FP8), func=COPY, scale=row_scale[s][:, b : b + 1]
+                )
+
+        def turn(s):
+            turned[s] = psum.tile([P, PASSES, 2, P], F32, tag="turn", name="turned")
+            words = wide[s][:].bitcast(F32)
+            for g in range(PASSES):
+                for u in range(2):
+                    if s < PACK:
+                        src = words[:, 2 * P * g + P * u : 2 * P * g + P * (u + 1)]
+                    else:
+                        src = words[:, 2 * P * g + u : 2 * P * (g + 1) : 2]
+                    nc.tensor.transpose(turned[s][:, g, u, :], src, ident[:])
+
+        def new_grouped(s0, count):
+            tile = flow.tile([P, count * R], BF16, tag="grouped", name="grouped", bufs=3, align_bytes=64)
+            for i in range(count):
+                grouped[s0 + i] = (tile, i)
+
+        def empty_turned(s):
+            tile, i = grouped[s]
+            nc.scalar.copy(
+                out=tile[:, i * R : (i + 1) * R].bitcast(F32).rearrange("p (g r u) -> p g r u", g=PASSES, u=2),
+                in_=turned[s][:].rearrange("p g u r -> p g r u"),
+            )
+
+        def quantize_cache(s0, count):
+            width = count * PASSES * P
+            codes = keep.tile([P, width], U32, name="c_codes%d" % s0, align_bytes=64)
+            plane = keep.tile([P, width], U8, name="c_plane%d" % s0, align_bytes=64)
+            nc.vector.quantize_mx(out=codes[:].bitcast(FP8X4), scales=plane[:], in_=grouped[s0][0][:])
+            for i in range(count):
+                c_codes[s0 + i] = codes[:, i * PASSES * P : (i + 1) * PASSES * P]
+                c_planes[s0 + i] = plane[:, i * PASSES * P : (i + 1) * PASSES * P]
+
+        banks = {}
+
+        def multiply(h, t, c):
+            g, j = divmod(h, 2)
+            s = PACK * g + t
+            banks[h, t, c] = psum.tile([P, N], F32, tag="acc", name="acc", bufs=6)
+            for k in range(PASSES):
+                nc.tensor.matmul_mx(
+                    out=banks[h, t, c][:],
+                    lhsT=c_codes[s][:, k * P : (k + 1) * P].bitcast(FP8X4),
+                    lhsT_scale=c_planes[s][:, k * P : (k + 1) * P],
+                    rhs=w_words[j][:, k, 2 * N * c : 2 * N * (c + 1)].bitcast(FP4X4),
+                    rhs_scale=w_scales[j][:, k, N * c : N * (c + 1)],
+                    start=(k == 0),
+                    stop=(k == PASSES - 1),
+                )
+
+        def add_bias(h, t, c):
+            j = h % 2
+            if h not in y_f32:
+                y_f32[h] = flow.tile([P, PACK, F], F32, tag="y_f32", name="y_f32", bufs=5)
+            nc.vector.tensor_tensor(
+                out=y_f32[h][:, t, N * c : N * (c + 1)],
+                in0=banks[h, t, c][:],
+                in1=bias[:, j * F + N * c : j * F + N * (c + 1)],
+                op=ADD,
+            )
+
+        def bank_step(h, t, c):
+            multiply(h, t, c)
+            add_bias(h, t, c)
+
+        def store_y(h, t0, t1, c0, c1):
+            g, j = divmod(h, 2)
+            nc.sync.dma_start(
+                out=y_rows[g][j][:, t0:t1, N * c0 : N * c1], in_=y_f32[h][:, t0:t1, N * c0 : N * c1]
+            )
+
+        def new_y_bf16(h, c, tag, bufs):
+            y_bf16[h, c] = flow.tile([P, N * PACK], BF16, tag=tag, name=tag, bufs=bufs, align_bytes=64)
+
+        def round_views(h, c, m0, m1):
+            src = y_f32[h][:, :, N * c + m0 : N * c + m1]
+            dst = y_bf16[h, c][:, PACK * m0 : PACK * m1]
+            return (
+                dst.rearrange("p (m i t) -> p m t i", i=RUN, t=PACK),
+                src.rearrange("p t (m i) -> p m t i", i=RUN),
+            )
+
+        def round_on_scalar(h, c, m0, m1):
+            dst, src = round_views(h, c, m0, m1)
+            nc.scalar.copy(out=dst, in_=src)
+
+        def round_on_vector(h, c, m0, m1):
+            dst, src = round_views(h, c, m0, m1)
+            nc.vector.tensor_copy(out=dst, in_=src)
+
+        def round_on_gpsimd(h, c):
+            nc.gpsimd.tensor_scalar(
+                out=y_bf16[h, c][:].rearrange("p (m t) -> p m t", t=PACK),
+                in0=y_f32[h][:, :, N * c : N * (c + 1)].rearrange("p t m -> p m t"),
+                scalar1=1.0,
+                scalar2=0.0,
+                op0=MULT,
+                op1=ADD,
+            )
+
+        def quantize_y(h, c):
+            g, j = divmod(h, 2)
+            if h not in y_codes:
+                y_codes[h] = flow.tile([P, F], U32, tag="y_codes", name="y_codes", bufs=3, align_bytes=64)
+            if g not in y_planes:
+                y_planes[g] = flow.tile([P, 2 * F], U8, tag="y_plane", name="y_plane", align_bytes=64)
+            nc.vector.quantize_mx(
+                out=y_codes[h][:, N * c : N * (c + 1)].bitcast(FP8X4),
+                scales=y_planes[g][:, j * F + N * c : j * F + N * (c + 1)],
+                in_=y_bf16[h, c][:],
+            )
+
+        def store_codes(h, c0, c1):
+            g, j = divmod(h, 2)
+            nc.sync.dma_start(
+                out=y_words[g][:, j * F + N * c0 : j * F + N * c1], in_=y_codes[h][:, N * c0 : N * c1].bitcast(I32)
+            )
+
+        def store_plane(g):
+            for q in range(4):
+                nc.sync.dma_start(
+                    out=y_scales[g, 4 * q : 4 * q + 4, :], in_=y_planes[g][32 * q : 32 * q + 4, :].bitcast(I32)
+                )
+
+        def round_half(h):
+            new_y_bf16(h, 0, "y_bf16_s", 2)
+            round_on_scalar(h, 0, 0, N)
+            new_y_bf16(h, 1, "y_bf16_g", 1)
+            round_on_gpsimd(h, 1)
+
+        def finish_half(h):
+            quantize_y(h, 0)
+            quantize_y(h, 1)
+            store_codes(h, 0, CHUNKS)
+            if h % 2 == 1:
+                store_plane(h // 2)
+
+        def head_slot(s):
+            turn(s)
+            new_grouped(s, 1)
+            empty_turned(s)
+
+        widen_on_vector(0)
+        head_slot(0)
+        widen_on_vector(1)
+        head_slot(1)
+        widen_on_vector(2)
+        quantize_cache(0, 1)
+        spread_bias(0)
+        multiply(0, 0, 0)
+        multiply(0, 0, 1)
+        head_slot(2)
+        widen_on_vector(3)
+        quantize_cache(1, 1)
+        multiply(0, 1, 0)
+        multiply(0, 1, 1)
+        head_slot(3)
+        add_bias(0, 0, 0)
+        quantize_cache(2, 1)
+        add_bias(0, 0, 1)
+        quantize_cache(3, 1)
+        add_bias(0, 1, 0)
+        add_bias(0, 1, 1)
+        widen_on_scalar(PACK)
+        widen_on_scalar(PACK + 1)
+
+        for h in range(HALVES - 1):
+            s = 2 * h + PACK
+            if h > 0:
+                round_half(h - 1)
+                for t in range(2):
+                    for c in range(CHUNKS):
+                        bank_step(h, t, c)
+            store_y(h, 0, 2, 0, CHUNKS)
+            if h == 0:
+                for c in range(CHUNKS):
+                    bank_step(h, 2, c)
+                spread_bias(1)
+            if s < SLOTS:
+                new_grouped(s, 2)
+                for i in range(2):
+                    turn(s + i)
+                for i in range(2):
+                    empty_turned(s + i)
+            for t in range(3 if h == 0 else 2, PACK):
+                for c in range(CHUNKS):
+                    bank_step(h, t, c)
+            store_y(h, 2, PACK, 0, CHUNKS)
+            if s + 2 < SLOTS:
+                widen_on_scalar(s + 2)
+                widen_on_scalar(s + 3)
+            if s < SLOTS:
+                quantize_cache(s, 2)
+            if h > 0:
+                finish_half(h - 1)
+
+        h = HALVES - 1
+        round_half(h - 1)
+        for t in range(PACK):
+            bank_step(h, t, 0)
+        store_y(h, 0, PACK, 0, 1)
+        new_y_bf16(h, 0, "y_bf16_s", 2)
+        round_on_scalar(h, 0, 0, N)
+        for t in range(2):
+            bank_step(h, t, 1)
+        store_y(h, 0, 2, 1, 2)
+        finish_half(h - 1)
+        for t in range(2, PACK):
+            bank_step(h, t, 1)
+        store_y(h, 2, PACK, 1, 2)
+        new_y_bf16(h, 1, "y_bf16_s", 2)
+        round_on_scalar(h, 1, 0, N // 2)
+        round_on_vector(h, 1, N // 2, N)
+        quantize_y(h, 0)
+        store_codes(h, 0, 1)
+        quantize_y(h, 1)
+        store_codes(h, 1, 2)
+        store_plane(GROUPS - 1)

@@ -27,7 +27,7 @@ BLOCKS = R // BLOCK
 N = 512
 CHUNKS = F // N
 HALVES = 2 * GROUPS
-RUN = 4
+RUN = 2
 
 FLOPS = 2 * S * R * 2 * F
 
@@ -49,7 +49,6 @@ def tile_latent_cache_key_value_b2_kernel(
         ctx.enter_context(tc.manual_schedule())
 
         ident = keep.tile([P, P], F32, name="ident")
-        make_identity(nc, ident[:])
         bias = keep.tile([P, 2 * F], BF16, name="bias")
         w_words, w_scales, bias_words = [], [], []
         for j in range(2):
@@ -57,6 +56,8 @@ def tile_latent_cache_key_value_b2_kernel(
             w_scales.append(keep.tile([P, PASSES, F], U8, name="w_scales%d" % j, align_bytes=64))
             bias_words.append(keep.tile([P, F // P], BF16, name="bias_words%d" % j))
             nc.vector.memset(w_scales[j][:].rearrange("p g n -> p (g n)").bitcast(I32), 0)
+        nc.vector.memset(ident[:], 0.0)
+        make_identity(nc, ident[:], nomemset=True)
 
         raw, row_scale = {}, {}
 
@@ -79,28 +80,28 @@ def tile_latent_cache_key_value_b2_kernel(
                 out=w_words[j][:].bitcast(I32), in_=words.rearrange("g p n -> p g n").bitcast(I32)
             )
 
-        def load_w_scales(j):
+        def load_w_scales(queue, j):
             scales = (k_scales, v_scales)[j]
             for q in range(4):
-                nc.sync.dma_start(
+                queue.dma_start(
                     out=w_scales[j][32 * q : 32 * q + 4, :, :].bitcast(I32),
                     in_=scales[:, 4 * q : 4 * q + 4, :].rearrange("g r n -> r g n").bitcast(I32),
                 )
 
-        def load_bias(j):
+        def load_bias(queue, j):
             row = (k_bias, v_bias)[j]
-            nc.sync.dma_start(out=bias_words[j][:], in_=row.rearrange("o (p e) -> p (o e)", p=P))
+            queue.dma_start(out=bias_words[j][:], in_=row.rearrange("o (p e) -> p (o e)", p=P))
 
         load_row_scales(nc.scalar, 0, 1)
         load_bytes(0, 0, 1)
-        load_w_scales(0)
         load_bytes(0, 1, PACK)
         load_w_words(0)
-        load_bias(0)
+        load_bias(nc.scalar, 0)
+        load_w_scales(nc.scalar, 0)
         load_bytes(1, 0, PACK)
         load_row_scales(nc.sync, 1, GROUPS)
-        load_w_scales(1)
-        load_bias(1)
+        load_bias(nc.sync, 1)
+        load_w_scales(nc.sync, 1)
         load_w_words(1)
         for g in range(2, GROUPS):
             load_bytes(g, 0, PACK)
@@ -109,7 +110,7 @@ def tile_latent_cache_key_value_b2_kernel(
         y_f32, y_bf16, y_codes, y_planes = {}, {}, {}, {}
 
         def spread_bias(j):
-            bank = psum.tile([P, PACK, P], F32, tag="turn", name="bias_bank")
+            bank = psum.tile([P, PACK, P], F32, tag="acc", name="bias_bank", bufs=6)
             words = bias_words[j][:].bitcast(F32)
             for e in range(PACK):
                 nc.tensor.transpose(bank[:, e, :], words[:, e : e + 1].to_broadcast([P, P]), ident[:])
@@ -118,7 +119,10 @@ def tile_latent_cache_key_value_b2_kernel(
                 in_=bank[:].rearrange("p e n -> p n e"),
             )
 
+        sorted_slots = set()
+
         def widen_on_vector(s):
+            sorted_slots.add(s)
             wide[s] = flow.tile([P, R], BF16, tag="wide", name="wide", bufs=4)
             sorted_view = wide[s][:].rearrange("p (g u q e) -> p g q u e", g=PASSES, u=2, e=2)
             for b in range(BLOCKS):
@@ -144,14 +148,14 @@ def tile_latent_cache_key_value_b2_kernel(
             words = wide[s][:].bitcast(F32)
             for g in range(PASSES):
                 for u in range(2):
-                    if s < PACK:
+                    if s in sorted_slots:
                         src = words[:, 2 * P * g + P * u : 2 * P * g + P * (u + 1)]
                     else:
                         src = words[:, 2 * P * g + u : 2 * P * (g + 1) : 2]
                     nc.tensor.transpose(turned[s][:, g, u, :], src, ident[:])
 
-        def new_grouped(s0, count):
-            tile = flow.tile([P, count * R], BF16, tag="grouped", name="grouped", bufs=3, align_bytes=64)
+        def new_grouped(s0, count, tag="grouped", bufs=3):
+            tile = flow.tile([P, count * R], BF16, tag=tag, name="grouped", bufs=bufs, align_bytes=64)
             for i in range(count):
                 grouped[s0 + i] = (tile, i)
 
@@ -199,9 +203,15 @@ def tile_latent_cache_key_value_b2_kernel(
                 op=ADD,
             )
 
-        def bank_step(h, t, c):
-            multiply(h, t, c)
-            add_bias(h, t, c)
+        def bank_pair(h, first, second):
+            multiply(h, *first)
+            multiply(h, *second)
+            add_bias(h, *second)
+            add_bias(h, *first)
+
+        def slot_step(h, t):
+            bank_pair(h, (t, 0), (t, 1))
+            store_y(h, t, t + 1, 0, CHUNKS)
 
         def store_y(h, t0, t1, c0, c1):
             g, j = divmod(h, 2)
@@ -256,9 +266,9 @@ def tile_latent_cache_key_value_b2_kernel(
                 out=y_words[g][:, j * F + N * c0 : j * F + N * c1], in_=y_codes[h][:, N * c0 : N * c1].bitcast(I32)
             )
 
-        def store_plane(g):
+        def store_plane(queue, g):
             for q in range(4):
-                nc.sync.dma_start(
+                queue.dma_start(
                     out=y_scales[g, 4 * q : 4 * q + 4, :], in_=y_planes[g][32 * q : 32 * q + 4, :].bitcast(I32)
                 )
 
@@ -269,84 +279,86 @@ def tile_latent_cache_key_value_b2_kernel(
             round_on_gpsimd(h, 1)
 
         def finish_half(h):
-            quantize_y(h, 0)
             quantize_y(h, 1)
             store_codes(h, 0, CHUNKS)
             if h % 2 == 1:
-                store_plane(h // 2)
+                store_plane(nc.sync, h // 2)
 
         def head_slot(s):
             turn(s)
             new_grouped(s, 1)
             empty_turned(s)
 
+        def turn_pair(s):
+            for i in range(2):
+                turn(s + i)
+            for i in range(2):
+                empty_turned(s + i)
+
+        spread_bias(0)
         widen_on_vector(0)
         head_slot(0)
         widen_on_vector(1)
         head_slot(1)
         widen_on_vector(2)
         quantize_cache(0, 1)
-        spread_bias(0)
-        multiply(0, 0, 0)
-        multiply(0, 0, 1)
         head_slot(2)
         widen_on_vector(3)
         quantize_cache(1, 1)
+        multiply(0, 0, 0)
+        multiply(0, 0, 1)
+        head_slot(3)
+        widen_on_scalar(PACK)
+        quantize_cache(2, 1)
+        add_bias(0, 0, 0)
+        add_bias(0, 0, 1)
+        store_y(0, 0, 1, 0, CHUNKS)
         multiply(0, 1, 0)
         multiply(0, 1, 1)
-        head_slot(3)
-        add_bias(0, 0, 0)
-        quantize_cache(2, 1)
-        add_bias(0, 0, 1)
-        quantize_cache(3, 1)
         add_bias(0, 1, 0)
+        quantize_cache(3, 1)
         add_bias(0, 1, 1)
-        widen_on_scalar(PACK)
+        store_y(0, 1, 2, 0, CHUNKS)
         widen_on_scalar(PACK + 1)
+        for t in range(2, PACK):
+            for c in range(CHUNKS):
+                multiply(0, t, c)
+                add_bias(0, t, c)
+            store_y(0, t, t + 1, 0, CHUNKS)
+        spread_bias(1)
+        new_grouped(PACK, 2, "y_bf16_g", 1)
+        turn_pair(PACK)
+        widen_on_vector(PACK + 2)
+        widen_on_vector(PACK + 3)
+        quantize_cache(PACK, 2)
 
-        for h in range(HALVES - 1):
+        for h in range(1, HALVES - 1):
             s = 2 * h + PACK
-            if h > 0:
-                round_half(h - 1)
-                for t in range(2):
-                    for c in range(CHUNKS):
-                        bank_step(h, t, c)
-            store_y(h, 0, 2, 0, CHUNKS)
-            if h == 0:
-                for c in range(CHUNKS):
-                    bank_step(h, 2, c)
-                spread_bias(1)
-            if s < SLOTS:
-                new_grouped(s, 2)
-                for i in range(2):
-                    turn(s + i)
-                for i in range(2):
-                    empty_turned(s + i)
-            for t in range(3 if h == 0 else 2, PACK):
-                for c in range(CHUNKS):
-                    bank_step(h, t, c)
-            store_y(h, 2, PACK, 0, CHUNKS)
+            round_half(h - 1)
             if s + 2 < SLOTS:
                 widen_on_scalar(s + 2)
                 widen_on_scalar(s + 3)
+            for t in range(PACK):
+                slot_step(h, t)
+            quantize_y(h - 1, 0)
             if s < SLOTS:
+                new_grouped(s, 2)
+                turn_pair(s)
                 quantize_cache(s, 2)
-            if h > 0:
-                finish_half(h - 1)
+            finish_half(h - 1)
 
         h = HALVES - 1
         round_half(h - 1)
-        for t in range(PACK):
-            bank_step(h, t, 0)
-        store_y(h, 0, PACK, 0, 1)
+        for t in range(0, PACK, 2):
+            bank_pair(h, (t, 0), (t + 1, 0))
+            store_y(h, t, t + 2, 0, 1)
         new_y_bf16(h, 0, "y_bf16_s", 2)
         round_on_scalar(h, 0, 0, N)
-        for t in range(2):
-            bank_step(h, t, 1)
+        bank_pair(h, (0, 1), (1, 1))
         store_y(h, 0, 2, 1, 2)
+        quantize_y(h - 1, 0)
         finish_half(h - 1)
-        for t in range(2, PACK):
-            bank_step(h, t, 1)
+        bank_pair(h, (2, 1), (3, 1))
         store_y(h, 2, PACK, 1, 2)
         new_y_bf16(h, 1, "y_bf16_s", 2)
         round_on_scalar(h, 1, 0, N // 2)
@@ -355,4 +367,4 @@ def tile_latent_cache_key_value_b2_kernel(
         store_codes(h, 0, 1)
         quantize_y(h, 1)
         store_codes(h, 1, 2)
-        store_plane(GROUPS - 1)
+        store_plane(nc.scalar, GROUPS - 1)

@@ -27,7 +27,9 @@ BLOCKS = R // BLOCK
 N = 512
 CHUNKS = F // N
 HALVES = 2 * GROUPS
-RUN = 2
+RUN = 4
+GPSIMD_COLS = 352
+WIDEN_STEPS = 5
 
 FLOPS = 2 * S * R * 2 * F
 
@@ -107,7 +109,8 @@ def tile_latent_cache_key_value_b2_kernel(
             load_bytes(g, 0, PACK)
 
         wide, turned, grouped, c_codes, c_planes = {}, {}, {}, {}, {}
-        y_f32, y_bf16, y_codes, y_planes = {}, {}, {}, {}
+        y_f32, y_bf16, y_codes = {}, {}, {}
+        y_plane = keep.tile([P, 2 * F], U8, name="y_plane", align_bytes=64)
 
         def spread_bias(j):
             bank = psum.tile([P, PACK, P], F32, tag="acc", name="bias_bank", bufs=6)
@@ -123,7 +126,7 @@ def tile_latent_cache_key_value_b2_kernel(
 
         def widen_on_vector(s):
             sorted_slots.add(s)
-            wide[s] = flow.tile([P, R], BF16, tag="wide", name="wide", bufs=4)
+            wide[s] = flow.tile([P, R], BF16, tag="wide", name="wide", bufs=5)
             sorted_view = wide[s][:].rearrange("p (g u q e) -> p g q u e", g=PASSES, u=2, e=2)
             for b in range(BLOCKS):
                 g, q0 = b // PACK, 32 * (b % PACK)
@@ -135,9 +138,11 @@ def tile_latent_cache_key_value_b2_kernel(
                     op0=MULT,
                 )
 
-        def widen_on_scalar(s):
-            wide[s] = flow.tile([P, R], BF16, tag="wide", name="wide", bufs=4)
-            for b in range(BLOCKS):
+        def widen_on_scalar(first, last):
+            for n in range(first, last):
+                s, b = divmod(n, BLOCKS)
+                if b == 0:
+                    wide[s] = flow.tile([P, R], BF16, tag="wide", name="wide", bufs=5)
                 cols = slice(b * BLOCK, (b + 1) * BLOCK)
                 nc.scalar.activation(
                     out=wide[s][:, cols], in_=raw[s][:, cols].bitcast(FP8), func=COPY, scale=row_scale[s][:, b : b + 1]
@@ -238,10 +243,10 @@ def tile_latent_cache_key_value_b2_kernel(
             dst, src = round_views(h, c, m0, m1)
             nc.vector.tensor_copy(out=dst, in_=src)
 
-        def round_on_gpsimd(h, c):
+        def round_on_gpsimd(h, c, m0, m1):
             nc.gpsimd.tensor_scalar(
-                out=y_bf16[h, c][:].rearrange("p (m t) -> p m t", t=PACK),
-                in0=y_f32[h][:, :, N * c : N * (c + 1)].rearrange("p t m -> p m t"),
+                out=y_bf16[h, c][:, PACK * m0 : PACK * m1].rearrange("p (m t) -> p m t", t=PACK),
+                in0=y_f32[h][:, :, N * c + m0 : N * c + m1].rearrange("p t m -> p m t"),
                 scalar1=1.0,
                 scalar2=0.0,
                 op0=MULT,
@@ -252,11 +257,9 @@ def tile_latent_cache_key_value_b2_kernel(
             g, j = divmod(h, 2)
             if h not in y_codes:
                 y_codes[h] = flow.tile([P, F], U32, tag="y_codes", name="y_codes", bufs=3, align_bytes=64)
-            if g not in y_planes:
-                y_planes[g] = flow.tile([P, 2 * F], U8, tag="y_plane", name="y_plane", align_bytes=64)
             nc.vector.quantize_mx(
                 out=y_codes[h][:, N * c : N * (c + 1)].bitcast(FP8X4),
-                scales=y_planes[g][:, j * F + N * c : j * F + N * (c + 1)],
+                scales=y_plane[4 * g :, j * F + N * c : j * F + N * (c + 1)],
                 in_=y_bf16[h, c][:],
             )
 
@@ -266,23 +269,22 @@ def tile_latent_cache_key_value_b2_kernel(
                 out=y_words[g][:, j * F + N * c0 : j * F + N * c1], in_=y_codes[h][:, N * c0 : N * c1].bitcast(I32)
             )
 
-        def store_plane(queue, g):
+        def store_plane():
             for q in range(4):
-                queue.dma_start(
-                    out=y_scales[g, 4 * q : 4 * q + 4, :], in_=y_planes[g][32 * q : 32 * q + 4, :].bitcast(I32)
+                nc.scalar.dma_start(
+                    out=y_scales[:, 4 * q : 4 * q + 4, :], in_=y_plane[32 * q : 32 * q + 4 * GROUPS, :].bitcast(I32)
                 )
 
         def round_half(h):
             new_y_bf16(h, 0, "y_bf16_s", 2)
             round_on_scalar(h, 0, 0, N)
             new_y_bf16(h, 1, "y_bf16_g", 1)
-            round_on_gpsimd(h, 1)
+            round_on_gpsimd(h, 1, 0, GPSIMD_COLS)
+            round_on_scalar(h, 1, GPSIMD_COLS, N)
 
         def finish_half(h):
             quantize_y(h, 1)
             store_codes(h, 0, CHUNKS)
-            if h % 2 == 1:
-                store_plane(nc.sync, h // 2)
 
         def head_slot(s):
             turn(s)
@@ -308,7 +310,7 @@ def tile_latent_cache_key_value_b2_kernel(
         multiply(0, 0, 0)
         multiply(0, 0, 1)
         head_slot(3)
-        widen_on_scalar(PACK)
+        widen_on_scalar(PACK * BLOCKS, (PACK + 1) * BLOCKS)
         quantize_cache(2, 1)
         add_bias(0, 0, 0)
         add_bias(0, 0, 1)
@@ -319,7 +321,7 @@ def tile_latent_cache_key_value_b2_kernel(
         quantize_cache(3, 1)
         add_bias(0, 1, 1)
         store_y(0, 1, 2, 0, CHUNKS)
-        widen_on_scalar(PACK + 1)
+        widen_on_scalar((PACK + 1) * BLOCKS, (PACK + 2) * BLOCKS)
         for t in range(2, PACK):
             for c in range(CHUNKS):
                 multiply(0, t, c)
@@ -332,12 +334,15 @@ def tile_latent_cache_key_value_b2_kernel(
         widen_on_vector(PACK + 3)
         quantize_cache(PACK, 2)
 
+        def late_block(step):
+            late = (SLOTS - 2 * PACK) * BLOCKS
+            return 2 * PACK * BLOCKS + (late * step + WIDEN_STEPS - 1) // WIDEN_STEPS
+
         for h in range(1, HALVES - 1):
             s = 2 * h + PACK
             round_half(h - 1)
-            if s + 2 < SLOTS:
-                widen_on_scalar(s + 2)
-                widen_on_scalar(s + 3)
+            if h <= WIDEN_STEPS:
+                widen_on_scalar(late_block(h - 1), late_block(h))
             for t in range(PACK):
                 slot_step(h, t)
             quantize_y(h - 1, 0)
@@ -367,4 +372,4 @@ def tile_latent_cache_key_value_b2_kernel(
         store_codes(h, 0, 1)
         quantize_y(h, 1)
         store_codes(h, 1, 2)
-        store_plane(nc.scalar, GROUPS - 1)
+        store_plane()

@@ -18,18 +18,21 @@ COPY = mybir.ActivationFunctionType.Copy
 S, R, F = 2048, 1024, 1024
 P = 128
 PACK = 4
-GROUP = P * PACK
-GROUPS = S // GROUP
+GROUPS = S // (P * PACK)
 SLOTS = GROUPS * PACK
-PASSES = R // GROUP
-BLOCK = 128
-BLOCKS = R // BLOCK
+PASSES = R // (P * PACK)
+SCALED = 128
+RUNS = R // SCALED
 N = 512
 CHUNKS = F // N
 HALVES = 2 * GROUPS
-RUN = 4
-GPSIMD_COLS = 352
+QUADRANTS = 4
+LINE = 4
+ACC_BANKS = 6
+WIDE_BUFS = 5
+GPSIMD_COLS = 416
 WIDEN_STEPS = 5
+LAST_SCALAR_COLS = 320
 
 FLOPS = 2 * S * R * 2 * F
 
@@ -38,7 +41,7 @@ def tile_latent_cache_key_value_b2_kernel(
     tc, C_bytes, C_scale, k_words, k_scales, v_words, v_scales, k_bias, v_bias, out_0, out_1, out_2
 ):
     nc = tc.nc
-    c_rows = C_bytes.rearrange("(g p t) k -> g p (t k)", p=P, t=PACK)
+    c_rows = C_bytes.rearrange("(g p t) r -> g p (t r)", p=P, t=PACK)
     c_scale_rows = C_scale.rearrange("(g p t) b -> p g (t b)", p=P, t=PACK)
     y_rows = out_0.rearrange("(g p t) j h d -> g j p t (h d)", p=P, t=PACK)
     y_words = out_1.rearrange("g p m t -> g p (m t)").bitcast(I32)
@@ -57,7 +60,7 @@ def tile_latent_cache_key_value_b2_kernel(
             w_words.append(keep.tile([P, PASSES, 2 * F], U8, name="w_words%d" % j, align_bytes=64))
             w_scales.append(keep.tile([P, PASSES, F], U8, name="w_scales%d" % j, align_bytes=64))
             bias_words.append(keep.tile([P, F // P], BF16, name="bias_words%d" % j))
-            nc.vector.memset(w_scales[j][:].rearrange("p g n -> p (g n)").bitcast(I32), 0)
+            nc.vector.memset(w_scales[j][:].rearrange("p k n -> p (k n)").bitcast(I32), 0)
         nc.vector.memset(ident[:], 0.0)
         make_identity(nc, ident[:], nomemset=True)
 
@@ -70,24 +73,24 @@ def tile_latent_cache_key_value_b2_kernel(
                 raw[PACK * g + t] = tile[:, (t - t0) * R : (t - t0 + 1) * R]
 
         def load_row_scales(queue, g0, g1):
-            tile = keep.tile([P, g1 - g0, PACK * BLOCKS], F32, name="row_scale%d" % g0)
+            tile = keep.tile([P, g1 - g0, PACK * RUNS], F32, name="row_scale%d" % g0)
             queue.dma_start(out=tile[:], in_=c_scale_rows[:, g0:g1, :])
             for g in range(g0, g1):
                 for t in range(PACK):
-                    row_scale[PACK * g + t] = tile[:, g - g0, t * BLOCKS : (t + 1) * BLOCKS]
+                    row_scale[PACK * g + t] = tile[:, g - g0, t * RUNS : (t + 1) * RUNS]
 
         def load_w_words(j):
             words = (k_words, v_words)[j]
             nc.sync.dma_start(
-                out=w_words[j][:].bitcast(I32), in_=words.rearrange("g p n -> p g n").bitcast(I32)
+                out=w_words[j][:].bitcast(I32), in_=words.rearrange("k p n -> p k n").bitcast(I32)
             )
 
         def load_w_scales(queue, j):
             scales = (k_scales, v_scales)[j]
-            for q in range(4):
+            for q in range(QUADRANTS):
                 queue.dma_start(
                     out=w_scales[j][32 * q : 32 * q + 4, :, :].bitcast(I32),
-                    in_=scales[:, 4 * q : 4 * q + 4, :].rearrange("g r n -> r g n").bitcast(I32),
+                    in_=scales[:, 4 * q : 4 * q + 4, :].rearrange("k r n -> r k n").bitcast(I32),
                 )
 
         def load_bias(queue, j):
@@ -108,12 +111,8 @@ def tile_latent_cache_key_value_b2_kernel(
         for g in range(2, GROUPS):
             load_bytes(g, 0, PACK)
 
-        wide, turned, grouped, c_codes, c_planes = {}, {}, {}, {}, {}
-        y_f32, y_bf16, y_codes = {}, {}, {}
-        y_plane = keep.tile([P, 2 * F], U8, name="y_plane", align_bytes=64)
-
         def spread_bias(j):
-            bank = psum.tile([P, PACK, P], F32, tag="acc", name="bias_bank", bufs=6)
+            bank = psum.tile([P, PACK, P], F32, tag="acc", name="bias_bank", bufs=ACC_BANKS)
             words = bias_words[j][:].bitcast(F32)
             for e in range(PACK):
                 nc.tensor.transpose(bank[:, e, :], words[:, e : e + 1].to_broadcast([P, P]), ident[:])
@@ -122,17 +121,19 @@ def tile_latent_cache_key_value_b2_kernel(
                 in_=bank[:].rearrange("p e n -> p n e"),
             )
 
+        wide, turned, grouped, c_codes, c_planes = {}, {}, {}, {}, {}
         sorted_slots = set()
 
         def widen_on_vector(s):
             sorted_slots.add(s)
-            wide[s] = flow.tile([P, R], BF16, tag="wide", name="wide", bufs=5)
-            sorted_view = wide[s][:].rearrange("p (g u q e) -> p g q u e", g=PASSES, u=2, e=2)
-            for b in range(BLOCKS):
-                g, q0 = b // PACK, 32 * (b % PACK)
+            wide[s] = flow.tile([P, R], BF16, tag="wide", name="wide", bufs=WIDE_BUFS)
+            sorted_view = wide[s][:].rearrange("p (k u q e) -> p k q u e", k=PASSES, u=2, e=2)
+            for b in range(RUNS):
+                k_pass, q0 = divmod(b * SCALED // PACK, P)
+                values = raw[s][:, b * SCALED : (b + 1) * SCALED].bitcast(FP8)
                 nc.vector.tensor_scalar(
-                    out=sorted_view[:, g, q0 : q0 + 32, :, :],
-                    in0=raw[s][:, b * BLOCK : (b + 1) * BLOCK].bitcast(FP8).rearrange("p (q u e) -> p q u e", u=2, e=2),
+                    out=sorted_view[:, k_pass, q0 : q0 + SCALED // PACK, :, :],
+                    in0=values.rearrange("p (q u e) -> p q u e", u=2, e=2),
                     scalar1=row_scale[s][:, b : b + 1],
                     scalar2=None,
                     op0=MULT,
@@ -140,10 +141,10 @@ def tile_latent_cache_key_value_b2_kernel(
 
         def widen_on_scalar(first, last):
             for n in range(first, last):
-                s, b = divmod(n, BLOCKS)
+                s, b = divmod(n, RUNS)
                 if b == 0:
-                    wide[s] = flow.tile([P, R], BF16, tag="wide", name="wide", bufs=5)
-                cols = slice(b * BLOCK, (b + 1) * BLOCK)
+                    wide[s] = flow.tile([P, R], BF16, tag="wide", name="wide", bufs=WIDE_BUFS)
+                cols = slice(b * SCALED, (b + 1) * SCALED)
                 nc.scalar.activation(
                     out=wide[s][:, cols], in_=raw[s][:, cols].bitcast(FP8), func=COPY, scale=row_scale[s][:, b : b + 1]
                 )
@@ -151,111 +152,115 @@ def tile_latent_cache_key_value_b2_kernel(
         def turn(s):
             turned[s] = psum.tile([P, PASSES, 2, P], F32, tag="turn", name="turned")
             words = wide[s][:].bitcast(F32)
-            for g in range(PASSES):
+            for k_pass in range(PASSES):
+                word0 = 2 * P * k_pass
                 for u in range(2):
                     if s in sorted_slots:
-                        src = words[:, 2 * P * g + P * u : 2 * P * g + P * (u + 1)]
+                        src = words[:, word0 + P * u : word0 + P * (u + 1)]
                     else:
-                        src = words[:, 2 * P * g + u : 2 * P * (g + 1) : 2]
-                    nc.tensor.transpose(turned[s][:, g, u, :], src, ident[:])
-
-        def new_grouped(s0, count, tag="grouped", bufs=3):
-            tile = flow.tile([P, count * R], BF16, tag=tag, name="grouped", bufs=bufs, align_bytes=64)
-            for i in range(count):
-                grouped[s0 + i] = (tile, i)
+                        src = words[:, word0 + u : word0 + 2 * P : 2]
+                    nc.tensor.transpose(turned[s][:, k_pass, u, :], src, ident[:])
 
         def empty_turned(s):
             tile, i = grouped[s]
             nc.scalar.copy(
-                out=tile[:, i * R : (i + 1) * R].bitcast(F32).rearrange("p (g r u) -> p g r u", g=PASSES, u=2),
-                in_=turned[s][:].rearrange("p g u r -> p g r u"),
+                out=tile[:, i * R : (i + 1) * R].bitcast(F32).rearrange("p (k r u) -> p k r u", k=PASSES, u=2),
+                in_=turned[s][:].rearrange("p k u r -> p k r u"),
             )
 
+        def turn_slots(s0, count, tag="grouped", bufs=3):
+            tile = flow.tile([P, count * R], BF16, tag=tag, name="grouped", bufs=bufs, align_bytes=64)
+            for i in range(count):
+                grouped[s0 + i] = (tile, i)
+                turn(s0 + i)
+            for i in range(count):
+                empty_turned(s0 + i)
+
         def quantize_cache(s0, count):
-            width = count * PASSES * P
-            codes = keep.tile([P, width], U32, name="c_codes%d" % s0, align_bytes=64)
-            plane = keep.tile([P, width], U8, name="c_plane%d" % s0, align_bytes=64)
+            width = PASSES * P
+            codes = keep.tile([P, count * width], U32, name="c_codes%d" % s0, align_bytes=64)
+            plane = keep.tile([P, count * width], U8, name="c_plane%d" % s0, align_bytes=64)
             nc.vector.quantize_mx(out=codes[:].bitcast(FP8X4), scales=plane[:], in_=grouped[s0][0][:])
             for i in range(count):
-                c_codes[s0 + i] = codes[:, i * PASSES * P : (i + 1) * PASSES * P]
-                c_planes[s0 + i] = plane[:, i * PASSES * P : (i + 1) * PASSES * P]
+                c_codes[s0 + i] = codes[:, i * width : (i + 1) * width]
+                c_planes[s0 + i] = plane[:, i * width : (i + 1) * width]
 
-        banks = {}
+        banks, y_half, y_chunk = {}, {}, {}
+
+        def new_y_half(h):
+            y_half[h] = flow.tile([P, PACK, F], F32, tag="y_f32", name="y_f32", bufs=5)
+            for c in range(CHUNKS):
+                y_chunk[h, c] = y_half[h][:, :, N * c : N * (c + 1)]
 
         def multiply(h, t, c):
             g, j = divmod(h, 2)
             s = PACK * g + t
-            banks[h, t, c] = psum.tile([P, N], F32, tag="acc", name="acc", bufs=6)
-            for k in range(PASSES):
+            banks[h, t, c] = psum.tile([P, N], F32, tag="acc", name="acc", bufs=ACC_BANKS)
+            for k_pass in range(PASSES):
                 nc.tensor.matmul_mx(
                     out=banks[h, t, c][:],
-                    lhsT=c_codes[s][:, k * P : (k + 1) * P].bitcast(FP8X4),
-                    lhsT_scale=c_planes[s][:, k * P : (k + 1) * P],
-                    rhs=w_words[j][:, k, 2 * N * c : 2 * N * (c + 1)].bitcast(FP4X4),
-                    rhs_scale=w_scales[j][:, k, N * c : N * (c + 1)],
-                    start=(k == 0),
-                    stop=(k == PASSES - 1),
+                    lhsT=c_codes[s][:, k_pass * P : (k_pass + 1) * P].bitcast(FP8X4),
+                    lhsT_scale=c_planes[s][:, k_pass * P : (k_pass + 1) * P],
+                    rhs=w_words[j][:, k_pass, 2 * N * c : 2 * N * (c + 1)].bitcast(FP4X4),
+                    rhs_scale=w_scales[j][:, k_pass, N * c : N * (c + 1)],
+                    start=(k_pass == 0),
+                    stop=(k_pass == PASSES - 1),
                 )
 
         def add_bias(h, t, c):
-            j = h % 2
-            if h not in y_f32:
-                y_f32[h] = flow.tile([P, PACK, F], F32, tag="y_f32", name="y_f32", bufs=5)
+            col0 = (h % 2) * F + N * c
             nc.vector.tensor_tensor(
-                out=y_f32[h][:, t, N * c : N * (c + 1)],
-                in0=banks[h, t, c][:],
-                in1=bias[:, j * F + N * c : j * F + N * (c + 1)],
-                op=ADD,
+                out=y_chunk[h, c][:, t, :], in0=banks[h, t, c][:], in1=bias[:, col0 : col0 + N], op=ADD
             )
 
-        def bank_pair(h, first, second):
-            multiply(h, *first)
-            multiply(h, *second)
-            add_bias(h, *second)
-            add_bias(h, *first)
+        def bank_pair(h, earlier, later):
+            multiply(h, *earlier)
+            multiply(h, *later)
+            add_bias(h, *later)
+            add_bias(h, *earlier)
 
-        def slot_step(h, t):
-            bank_pair(h, (t, 0), (t, 1))
-            store_y(h, t, t + 1, 0, CHUNKS)
-
-        def store_y(h, t0, t1, c0, c1):
+        def store_slot(h, t):
             g, j = divmod(h, 2)
-            nc.sync.dma_start(
-                out=y_rows[g][j][:, t0:t1, N * c0 : N * c1], in_=y_f32[h][:, t0:t1, N * c0 : N * c1]
-            )
+            nc.sync.dma_start(out=y_rows[g][j][:, t : t + 1, :], in_=y_half[h][:, t : t + 1, :])
+
+        def store_chunk(h, c, t0, t1):
+            g, j = divmod(h, 2)
+            nc.sync.dma_start(out=y_rows[g][j][:, t0:t1, N * c : N * (c + 1)], in_=y_chunk[h, c][:, t0:t1, :])
+
+        y_bf16, y_codes = {}, {}
+        y_plane = keep.tile([P, 2 * F], U8, name="y_plane", align_bytes=64)
 
         def new_y_bf16(h, c, tag, bufs):
             y_bf16[h, c] = flow.tile([P, N * PACK], BF16, tag=tag, name=tag, bufs=bufs, align_bytes=64)
 
-        def round_views(h, c, m0, m1):
-            src = y_f32[h][:, :, N * c + m0 : N * c + m1]
-            dst = y_bf16[h, c][:, PACK * m0 : PACK * m1]
-            return (
-                dst.rearrange("p (m i t) -> p m t i", i=RUN, t=PACK),
-                src.rearrange("p t (m i) -> p m t i", i=RUN),
+        def round_by_lines(copy, h, c, m0, m1):
+            copy(
+                out=y_bf16[h, c][:, PACK * m0 : PACK * m1].rearrange("p (m i t) -> p m t i", i=LINE, t=PACK),
+                in_=y_chunk[h, c][:, :, m0:m1].rearrange("p t (m i) -> p m t i", i=LINE),
             )
-
-        def round_on_scalar(h, c, m0, m1):
-            dst, src = round_views(h, c, m0, m1)
-            nc.scalar.copy(out=dst, in_=src)
-
-        def round_on_vector(h, c, m0, m1):
-            dst, src = round_views(h, c, m0, m1)
-            nc.vector.tensor_copy(out=dst, in_=src)
 
         def round_on_gpsimd(h, c, m0, m1):
             nc.gpsimd.tensor_scalar(
                 out=y_bf16[h, c][:, PACK * m0 : PACK * m1].rearrange("p (m t) -> p m t", t=PACK),
-                in0=y_f32[h][:, :, N * c + m0 : N * c + m1].rearrange("p t m -> p m t"),
+                in0=y_chunk[h, c][:, :, m0:m1].rearrange("p t m -> p m t"),
                 scalar1=1.0,
                 scalar2=0.0,
                 op0=MULT,
                 op1=ADD,
             )
 
+        def round_half(h):
+            new_y_bf16(h, 0, "y_bf16_s", 2)
+            round_by_lines(nc.scalar.copy, h, 0, 0, N)
+            new_y_bf16(h, 1, "y_bf16_g", 1)
+            round_on_gpsimd(h, 1, 0, GPSIMD_COLS)
+
+        def round_rest(h):
+            round_by_lines(nc.scalar.copy, h, 1, GPSIMD_COLS, N)
+
         def quantize_y(h, c):
             g, j = divmod(h, 2)
-            if h not in y_codes:
+            if c == 0:
                 y_codes[h] = flow.tile([P, F], U32, tag="y_codes", name="y_codes", bufs=3, align_bytes=64)
             nc.vector.quantize_mx(
                 out=y_codes[h][:, N * c : N * (c + 1)].bitcast(FP8X4),
@@ -269,107 +274,86 @@ def tile_latent_cache_key_value_b2_kernel(
                 out=y_words[g][:, j * F + N * c0 : j * F + N * c1], in_=y_codes[h][:, N * c0 : N * c1].bitcast(I32)
             )
 
-        def store_plane():
-            for q in range(4):
-                nc.scalar.dma_start(
-                    out=y_scales[:, 4 * q : 4 * q + 4, :], in_=y_plane[32 * q : 32 * q + 4 * GROUPS, :].bitcast(I32)
-                )
-
-        def round_half(h):
-            new_y_bf16(h, 0, "y_bf16_s", 2)
-            round_on_scalar(h, 0, 0, N)
-            new_y_bf16(h, 1, "y_bf16_g", 1)
-            round_on_gpsimd(h, 1, 0, GPSIMD_COLS)
-            round_on_scalar(h, 1, GPSIMD_COLS, N)
-
-        def finish_half(h):
-            quantize_y(h, 1)
-            store_codes(h, 0, CHUNKS)
-
-        def head_slot(s):
-            turn(s)
-            new_grouped(s, 1)
-            empty_turned(s)
-
-        def turn_pair(s):
-            for i in range(2):
-                turn(s + i)
-            for i in range(2):
-                empty_turned(s + i)
-
+        new_y_half(0)
         spread_bias(0)
         widen_on_vector(0)
-        head_slot(0)
+        turn_slots(0, 1)
         widen_on_vector(1)
-        head_slot(1)
+        turn_slots(1, 1)
         widen_on_vector(2)
         quantize_cache(0, 1)
-        head_slot(2)
+        turn_slots(2, 1)
         widen_on_vector(3)
         quantize_cache(1, 1)
         multiply(0, 0, 0)
         multiply(0, 0, 1)
-        head_slot(3)
-        widen_on_scalar(PACK * BLOCKS, (PACK + 1) * BLOCKS)
+        turn_slots(3, 1)
+        widen_on_scalar(PACK * RUNS, (PACK + 1) * RUNS)
         quantize_cache(2, 1)
         add_bias(0, 0, 0)
         add_bias(0, 0, 1)
-        store_y(0, 0, 1, 0, CHUNKS)
+        store_slot(0, 0)
         multiply(0, 1, 0)
         multiply(0, 1, 1)
         add_bias(0, 1, 0)
         quantize_cache(3, 1)
         add_bias(0, 1, 1)
-        store_y(0, 1, 2, 0, CHUNKS)
-        widen_on_scalar((PACK + 1) * BLOCKS, (PACK + 2) * BLOCKS)
+        store_slot(0, 1)
+        widen_on_scalar((PACK + 1) * RUNS, (PACK + 2) * RUNS)
         for t in range(2, PACK):
             for c in range(CHUNKS):
                 multiply(0, t, c)
                 add_bias(0, t, c)
-            store_y(0, t, t + 1, 0, CHUNKS)
+            store_slot(0, t)
         spread_bias(1)
-        new_grouped(PACK, 2, "y_bf16_g", 1)
-        turn_pair(PACK)
+        turn_slots(PACK, 2, "y_bf16_g", 1)
         widen_on_vector(PACK + 2)
         widen_on_vector(PACK + 3)
         quantize_cache(PACK, 2)
 
-        def late_block(step):
-            late = (SLOTS - 2 * PACK) * BLOCKS
-            return 2 * PACK * BLOCKS + (late * step + WIDEN_STEPS - 1) // WIDEN_STEPS
+        def widened_after(step):
+            left = (SLOTS - 2 * PACK) * RUNS
+            return 2 * PACK * RUNS + (left * step + WIDEN_STEPS - 1) // WIDEN_STEPS
 
         for h in range(1, HALVES - 1):
             s = 2 * h + PACK
             round_half(h - 1)
             if h <= WIDEN_STEPS:
-                widen_on_scalar(late_block(h - 1), late_block(h))
+                widen_on_scalar(widened_after(h - 1), widened_after(h))
+            new_y_half(h)
             for t in range(PACK):
-                slot_step(h, t)
+                bank_pair(h, (t, 0), (t, 1))
+                store_slot(h, t)
             quantize_y(h - 1, 0)
             if s < SLOTS:
-                new_grouped(s, 2)
-                turn_pair(s)
+                turn_slots(s, 2)
                 quantize_cache(s, 2)
-            finish_half(h - 1)
+            round_rest(h - 1)
+            quantize_y(h - 1, 1)
+            store_codes(h - 1, 0, CHUNKS)
 
         h = HALVES - 1
         round_half(h - 1)
-        for t in range(0, PACK, 2):
-            bank_pair(h, (t, 0), (t + 1, 0))
-            store_y(h, t, t + 2, 0, 1)
-        new_y_bf16(h, 0, "y_bf16_s", 2)
-        round_on_scalar(h, 0, 0, N)
-        bank_pair(h, (0, 1), (1, 1))
-        store_y(h, 0, 2, 1, 2)
-        quantize_y(h - 1, 0)
-        finish_half(h - 1)
-        bank_pair(h, (2, 1), (3, 1))
-        store_y(h, 2, PACK, 1, 2)
-        new_y_bf16(h, 1, "y_bf16_s", 2)
-        round_on_scalar(h, 1, 0, N // 2)
-        round_on_vector(h, 1, N // 2, N)
-        quantize_y(h, 0)
-        store_codes(h, 0, 1)
-        quantize_y(h, 1)
-        store_codes(h, 1, 2)
-        store_plane()
+        round_rest(h - 1)
+        for c in range(CHUNKS):
+            tile = keep.tile([P, PACK, N], F32, name="y_last%d" % c)
+            y_chunk[h, c] = tile[:]
+            for t in range(0, PACK, 2):
+                bank_pair(h, (t, c), (t + 1, c))
+                store_chunk(h, c, t, t + 2)
+            if c == 0:
+                new_y_bf16(h, 0, "y_bf16_s", 2)
+                round_by_lines(nc.scalar.copy, h, 0, 0, N)
+        for c in range(CHUNKS):
+            quantize_y(h - 1, c)
+        store_codes(h - 1, 0, CHUNKS)
+        new_y_bf16(h, 1, "y_bf16_last", 1)
+        round_by_lines(nc.scalar.copy, h, 1, 0, LAST_SCALAR_COLS)
+        round_by_lines(nc.vector.tensor_copy, h, 1, LAST_SCALAR_COLS, N)
+        for c in range(CHUNKS):
+            quantize_y(h, c)
+            store_codes(h, c, c + 1)
+        for q in range(QUADRANTS):
+            nc.scalar.dma_start(
+                out=y_scales[:, 4 * q : 4 * q + 4, :], in_=y_plane[32 * q : 32 * q + 4 * GROUPS, :].bitcast(I32)
+            )

@@ -30,7 +30,7 @@ QUADRANTS = 4
 LINE = 4
 ACC_BANKS = 6
 WIDE_BUFS = 5
-GPSIMD_COLS = 416
+GPSIMD_COLS = 512
 WIDEN_STEPS = 5
 LAST_SCALAR_COLS = 320
 
@@ -255,9 +255,6 @@ def tile_latent_cache_key_value_b2_kernel(
             new_y_bf16(h, 1, "y_bf16_g", 1)
             round_on_gpsimd(h, 1, 0, GPSIMD_COLS)
 
-        def round_rest(h):
-            round_by_lines(nc.scalar.copy, h, 1, GPSIMD_COLS, N)
-
         def quantize_y(h, c):
             g, j = divmod(h, 2)
             if c == 0:
@@ -328,13 +325,11 @@ def tile_latent_cache_key_value_b2_kernel(
             if s < SLOTS:
                 turn_slots(s, 2)
                 quantize_cache(s, 2)
-            round_rest(h - 1)
             quantize_y(h - 1, 1)
             store_codes(h - 1, 0, CHUNKS)
 
         h = HALVES - 1
         round_half(h - 1)
-        round_rest(h - 1)
         for c in range(CHUNKS):
             tile = keep.tile([P, PACK, N], F32, name="y_last%d" % c)
             y_chunk[h, c] = tile[:]

@@ -14,6 +14,7 @@ FP4X4 = mybir.dt.float4_e2m1fn_x4
 ADD = mybir.AluOpType.add
 MULT = mybir.AluOpType.mult
 COPY = mybir.ActivationFunctionType.Copy
+IDENTITY = mybir.ActivationFunctionType.Identity
 
 S, R, F = 2048, 1024, 1024
 P = 128
@@ -29,7 +30,7 @@ HALVES = 2 * GROUPS
 QUADRANTS = 4
 LINE = 4
 ACC_BANKS = 6
-WIDE_BUFS = 5
+WIDE_BUFS = 8
 GPSIMD_COLS = 512
 WIDEN_STEPS = 5
 LAST_SCALAR_COLS = 320
@@ -97,6 +98,15 @@ def tile_latent_cache_key_value_b2_kernel(
             row = (k_bias, v_bias)[j]
             queue.dma_start(out=bias_words[j][:], in_=row.rearrange("o (p e) -> p (o e)", p=P))
 
+        bias_column = {}
+
+        def load_bias_column(j):
+            row = (k_bias, v_bias)[j]
+            tile = keep.tile([P, PACK, 2], BF16, name="bias_column%d" % j)
+            with nc.allow_non_contiguous_dma(reason="one bias value to a partition"):
+                nc.sync.dma_start(out=tile[:, :, 0:1], in_=row[:, 0:N].rearrange("o (b p) -> p b o", p=P))
+            bias_column[j] = tile
+
         load_row_scales(nc.scalar, 0, 1)
         load_bytes(0, 0, 1)
         load_bytes(0, 1, PACK)
@@ -105,11 +115,12 @@ def tile_latent_cache_key_value_b2_kernel(
         load_w_scales(nc.scalar, 0)
         load_bytes(1, 0, PACK)
         load_row_scales(nc.sync, 1, GROUPS)
+        load_bytes(2, 0, PACK)
         load_bias(nc.sync, 1)
         load_w_scales(nc.sync, 1)
         load_w_words(1)
-        for g in range(2, GROUPS):
-            load_bytes(g, 0, PACK)
+        load_bytes(3, 0, PACK)
+        load_bias_column(1)
 
         def spread_bias(j):
             bank = psum.tile([P, PACK, P], F32, tag="acc", name="bias_bank", bufs=ACC_BANKS)
@@ -120,6 +131,7 @@ def tile_latent_cache_key_value_b2_kernel(
                 out=bias[:, j * F : (j + 1) * F].bitcast(F32).rearrange("p (n e) -> p n e", e=PACK),
                 in_=bank[:].rearrange("p e n -> p n e"),
             )
+
 
         wide, turned, grouped, c_codes, c_planes = {}, {}, {}, {}, {}
         sorted_slots = set()
@@ -213,6 +225,35 @@ def tile_latent_cache_key_value_b2_kernel(
                 out=y_chunk[h, c][:, t, :], in0=banks[h, t, c][:], in1=bias[:, col0 : col0 + N], op=ADD
             )
 
+        across = {}
+
+        def multiply_across(h, t):
+            g, j = divmod(h, 2)
+            s = PACK * g + t
+            bank = psum.tile([P, PACK, P], F32, tag="acc", name="acc_across", bufs=ACC_BANKS)
+            for b in range(PACK):
+                for k_pass in range(PASSES):
+                    nc.tensor.matmul_mx(
+                        out=bank[:, b, :],
+                        lhsT=w_words[j][:, k_pass, 2 * P * b : 2 * P * (b + 1)].bitcast(FP4X4),
+                        lhsT_scale=w_scales[j][:, k_pass, P * b : P * (b + 1)],
+                        rhs=c_codes[s][:, k_pass * P : (k_pass + 1) * P].bitcast(FP8X4),
+                        rhs_scale=c_planes[s][:, k_pass * P : (k_pass + 1) * P],
+                        start=(k_pass == 0),
+                        stop=(k_pass == PASSES - 1),
+                    )
+            across[h] = flow.tile([P, PACK, P], F32, tag="across", name="across")
+            for b in range(PACK):
+                nc.scalar.activation(
+                    out=across[h][:, b, :], in_=bank[:, b, :], func=IDENTITY, bias=bias_column[j][:, b, 0:1]
+                )
+
+        def turn_back(h, t):
+            bank = psum.tile([P, PACK, P], F32, tag="acc", name="turned_back", bufs=ACC_BANKS)
+            for b in range(PACK):
+                nc.tensor.transpose(bank[:, b, :], across[h][:, b, :], ident[:])
+            nc.scalar.copy(out=y_chunk[h, 0][:, t, :], in_=bank[:].rearrange("p b n -> p (b n)"))
+
         def bank_pair(h, earlier, later):
             multiply(h, *earlier)
             multiply(h, *later)
@@ -258,7 +299,7 @@ def tile_latent_cache_key_value_b2_kernel(
         def quantize_y(h, c):
             g, j = divmod(h, 2)
             if c == 0:
-                y_codes[h] = flow.tile([P, F], U32, tag="y_codes", name="y_codes", bufs=3, align_bytes=64)
+                y_codes[h] = flow.tile([P, F], U32, tag="y_codes", name="y_codes", bufs=HALVES, align_bytes=64)
             nc.vector.quantize_mx(
                 out=y_codes[h][:, N * c : N * (c + 1)].bitcast(FP8X4),
                 scales=y_plane[4 * g :, j * F + N * c : j * F + N * (c + 1)],
@@ -284,10 +325,11 @@ def tile_latent_cache_key_value_b2_kernel(
         quantize_cache(1, 1)
         multiply(0, 0, 0)
         multiply(0, 0, 1)
+        widen_on_scalar(5 * RUNS, (5 + 1) * RUNS)
         turn_slots(3, 1)
-        widen_on_scalar(PACK * RUNS, (PACK + 1) * RUNS)
         quantize_cache(2, 1)
         add_bias(0, 0, 0)
+        widen_on_vector(4)
         add_bias(0, 0, 1)
         store_slot(0, 0)
         multiply(0, 1, 0)
@@ -296,37 +338,131 @@ def tile_latent_cache_key_value_b2_kernel(
         quantize_cache(3, 1)
         add_bias(0, 1, 1)
         store_slot(0, 1)
-        widen_on_scalar((PACK + 1) * RUNS, (PACK + 2) * RUNS)
-        for t in range(2, PACK):
-            for c in range(CHUNKS):
-                multiply(0, t, c)
-                add_bias(0, t, c)
-            store_slot(0, t)
+        widen_on_scalar(8 * RUNS, (8 + 1) * RUNS)
+        widen_on_scalar(9 * RUNS, (9 + 1) * RUNS)
+        multiply(0, 2, 0)
+        add_bias(0, 2, 0)
+        multiply(0, 2, 1)
+        add_bias(0, 2, 1)
+        store_slot(0, 2)
+        multiply(0, 3, 0)
+        add_bias(0, 3, 0)
+        multiply(0, 3, 1)
+        add_bias(0, 3, 1)
+        store_slot(0, 3)
         spread_bias(1)
         turn_slots(PACK, 2, "y_bf16_g", 1)
-        widen_on_vector(PACK + 2)
-        widen_on_vector(PACK + 3)
+        widen_on_scalar(10 * RUNS, (10 + 1) * RUNS)
+        widen_on_vector(6)
+        widen_on_vector(7)
         quantize_cache(PACK, 2)
+
 
         def widened_after(step):
             left = (SLOTS - 2 * PACK) * RUNS
             return 2 * PACK * RUNS + (left * step + WIDEN_STEPS - 1) // WIDEN_STEPS
 
-        for h in range(1, HALVES - 1):
-            s = 2 * h + PACK
-            round_half(h - 1)
-            if h <= WIDEN_STEPS:
-                widen_on_scalar(widened_after(h - 1), widened_after(h))
-            new_y_half(h)
-            for t in range(PACK):
-                bank_pair(h, (t, 0), (t, 1))
-                store_slot(h, t)
-            quantize_y(h - 1, 0)
-            if s < SLOTS:
-                turn_slots(s, 2)
-                quantize_cache(s, 2)
-            quantize_y(h - 1, 1)
-            store_codes(h - 1, 0, CHUNKS)
+        new_y_half(1)
+        multiply_across(1, 3)
+        round_half(0)
+        bank_pair(1, (0, 0), (0, 1))
+        store_slot(1, 0)
+        bank_pair(1, (1, 0), (1, 1))
+        store_slot(1, 1)
+        bank_pair(1, (2, 0), (2, 1))
+        store_slot(1, 2)
+        multiply(1, 3, 1)
+        add_bias(1, 3, 1)
+        quantize_y(0, 0)
+        turn_slots(6, 2)
+        turn_back(1, 3)
+        store_slot(1, 3)
+        quantize_cache(6, 2)
+        widen_on_scalar(88, 98)
+        quantize_y(0, 1)
+        store_codes(0, 0, CHUNKS)
+        new_y_half(2)
+        round_half(1)
+        bank_pair(2, (0, 0), (0, 1))
+        store_slot(2, 0)
+        bank_pair(2, (1, 0), (1, 1))
+        store_slot(2, 1)
+        bank_pair(2, (2, 0), (2, 1))
+        store_slot(2, 2)
+        bank_pair(2, (3, 0), (3, 1))
+        store_slot(2, 3)
+        quantize_y(1, 0)
+        turn_slots(8, 2)
+        quantize_cache(8, 2)
+        widen_on_scalar(98, 108)
+        quantize_y(1, 1)
+        store_codes(1, 0, CHUNKS)
+        new_y_half(3)
+        multiply_across(3, 3)
+        round_half(2)
+        bank_pair(3, (0, 0), (0, 1))
+        store_slot(3, 0)
+        bank_pair(3, (1, 0), (1, 1))
+        store_slot(3, 1)
+        bank_pair(3, (2, 0), (2, 1))
+        store_slot(3, 2)
+        multiply(3, 3, 1)
+        add_bias(3, 3, 1)
+        quantize_y(2, 0)
+        turn_slots(10, 2)
+        turn_back(3, 3)
+        store_slot(3, 3)
+        quantize_cache(10, 2)
+        widen_on_scalar(108, 118)
+        quantize_y(2, 1)
+        store_codes(2, 0, CHUNKS)
+        new_y_half(4)
+        round_half(3)
+        bank_pair(4, (0, 0), (0, 1))
+        store_slot(4, 0)
+        bank_pair(4, (1, 0), (1, 1))
+        store_slot(4, 1)
+        bank_pair(4, (2, 0), (2, 1))
+        store_slot(4, 2)
+        bank_pair(4, (3, 0), (3, 1))
+        store_slot(4, 3)
+        quantize_y(3, 0)
+        turn_slots(12, 2)
+        quantize_cache(12, 2)
+        widen_on_scalar(118, 128)
+        quantize_y(3, 1)
+        store_codes(3, 0, CHUNKS)
+        new_y_half(5)
+        multiply_across(5, 3)
+        round_half(4)
+        bank_pair(5, (0, 0), (0, 1))
+        store_slot(5, 0)
+        bank_pair(5, (1, 0), (1, 1))
+        store_slot(5, 1)
+        bank_pair(5, (2, 0), (2, 1))
+        store_slot(5, 2)
+        multiply(5, 3, 1)
+        add_bias(5, 3, 1)
+        quantize_y(4, 0)
+        turn_slots(14, 2)
+        turn_back(5, 3)
+        store_slot(5, 3)
+        quantize_cache(14, 2)
+        quantize_y(4, 1)
+        store_codes(4, 0, CHUNKS)
+        new_y_half(6)
+        round_half(5)
+        bank_pair(6, (0, 0), (0, 1))
+        store_slot(6, 0)
+        bank_pair(6, (1, 0), (1, 1))
+        store_slot(6, 1)
+        bank_pair(6, (2, 0), (2, 1))
+        store_slot(6, 2)
+        bank_pair(6, (3, 0), (3, 1))
+        store_slot(6, 3)
+        quantize_y(5, 0)
+        quantize_y(5, 1)
+        store_codes(5, 0, CHUNKS)
 
         h = HALVES - 1
         round_half(h - 1)

@@ -58,8 +58,8 @@ def tile_latent_cache_key_value_b2_kernel(
         bias = keep.tile([P, 2 * F], BF16, name="bias")
         w_words, w_scales, bias_words = [], [], []
         for j in range(2):
-            w_words.append(keep.tile([P, PASSES, 2 * F], U8, name="w_words%d" % j, align_bytes=64))
-            w_scales.append(keep.tile([P, PASSES, F], U8, name="w_scales%d" % j, align_bytes=64))
+            w_words.append(keep.tile([P, PASSES, 2 * F], U8, name="w_words%d" % j, align_bytes=256))
+            w_scales.append(keep.tile([P, PASSES, F], U8, name="w_scales%d" % j, align_bytes=256))
             bias_words.append(keep.tile([P, F // P], BF16, name="bias_words%d" % j))
             nc.vector.memset(w_scales[j][:].rearrange("p k n -> p (k n)").bitcast(I32), 0)
         nc.vector.memset(ident[:], 0.0)
@@ -190,8 +190,8 @@ def tile_latent_cache_key_value_b2_kernel(
 
         def quantize_cache(s0, count):
             width = PASSES * P
-            codes = keep.tile([P, count * width], U32, name="c_codes%d" % s0, align_bytes=64)
-            plane = keep.tile([P, count * width], U8, name="c_plane%d" % s0, align_bytes=64)
+            codes = keep.tile([P, count * width], U32, name="c_codes%d" % s0, align_bytes=256)
+            plane = keep.tile([P, count * width], U8, name="c_plane%d" % s0, align_bytes=256)
             nc.vector.quantize_mx(out=codes[:].bitcast(FP8X4), scales=plane[:], in_=grouped[s0][0][:])
             for i in range(count):
                 c_codes[s0 + i] = codes[:, i * width : (i + 1) * width]

@@ -31,8 +31,9 @@ QUADRANTS = 4
 LINE = 4
 ACC_BANKS = 6
 WIDE_BUFS = 8
-GPSIMD_COLS = 512
-WIDEN_STEPS = 5
+EARLY_SLOTS = 11
+WIDEN_STEPS = 4
+OPERAND_ALIGN = 256
 LAST_SCALAR_COLS = 320
 
 FLOPS = 2 * S * R * 2 * F
@@ -58,8 +59,8 @@ def tile_latent_cache_key_value_b2_kernel(
         bias = keep.tile([P, 2 * F], BF16, name="bias")
         w_words, w_scales, bias_words = [], [], []
         for j in range(2):
-            w_words.append(keep.tile([P, PASSES, 2 * F], U8, name="w_words%d" % j, align_bytes=256))
-            w_scales.append(keep.tile([P, PASSES, F], U8, name="w_scales%d" % j, align_bytes=256))
+            w_words.append(keep.tile([P, PASSES, 2 * F], U8, name="w_words%d" % j, align_bytes=OPERAND_ALIGN))
+            w_scales.append(keep.tile([P, PASSES, F], U8, name="w_scales%d" % j, align_bytes=OPERAND_ALIGN))
             bias_words.append(keep.tile([P, F // P], BF16, name="bias_words%d" % j))
             nc.vector.memset(w_scales[j][:].rearrange("p k n -> p (k n)").bitcast(I32), 0)
         nc.vector.memset(ident[:], 0.0)
@@ -73,9 +74,9 @@ def tile_latent_cache_key_value_b2_kernel(
             for t in range(t0, t1):
                 raw[PACK * g + t] = tile[:, (t - t0) * R : (t - t0 + 1) * R]
 
-        def load_row_scales(queue, g0, g1):
+        def load_row_scales(g0, g1):
             tile = keep.tile([P, g1 - g0, PACK * RUNS], F32, name="row_scale%d" % g0)
-            queue.dma_start(out=tile[:], in_=c_scale_rows[:, g0:g1, :])
+            nc.sync.dma_start(out=tile[:], in_=c_scale_rows[:, g0:g1, :])
             for g in range(g0, g1):
                 for t in range(PACK):
                     row_scale[PACK * g + t] = tile[:, g - g0, t * RUNS : (t + 1) * RUNS]
@@ -94,33 +95,30 @@ def tile_latent_cache_key_value_b2_kernel(
                     in_=scales[:, 4 * q : 4 * q + 4, :].rearrange("k r n -> r k n").bitcast(I32),
                 )
 
-        def load_bias(queue, j):
+        def load_bias(j):
             row = (k_bias, v_bias)[j]
-            queue.dma_start(out=bias_words[j][:], in_=row.rearrange("o (p e) -> p (o e)", p=P))
+            nc.sync.dma_start(out=bias_words[j][:], in_=row.rearrange("o (p e) -> p (o e)", p=P))
 
-        bias_column = {}
-
-        def load_bias_column(j):
-            row = (k_bias, v_bias)[j]
-            tile = keep.tile([P, PACK, 2], BF16, name="bias_column%d" % j)
+        def load_value_bias_columns():
+            tile = keep.tile([P, PACK, 2], BF16, name="bias_column1")
             with nc.allow_non_contiguous_dma(reason="one bias value to a partition"):
-                nc.sync.dma_start(out=tile[:, :, 0:1], in_=row[:, 0:N].rearrange("o (b p) -> p b o", p=P))
-            bias_column[j] = tile
+                nc.sync.dma_start(out=tile[:, :, 0:1], in_=v_bias[:, 0:N].rearrange("o (b p) -> p b o", p=P))
+            return tile
 
-        load_row_scales(nc.scalar, 0, 1)
+        load_bias(0)
+        load_row_scales(0, 1)
         load_bytes(0, 0, 1)
         load_bytes(0, 1, PACK)
         load_w_words(0)
-        load_bias(nc.scalar, 0)
         load_w_scales(nc.scalar, 0)
         load_bytes(1, 0, PACK)
-        load_row_scales(nc.sync, 1, GROUPS)
+        load_row_scales(1, GROUPS)
         load_bytes(2, 0, PACK)
-        load_bias(nc.sync, 1)
+        load_bias(1)
         load_w_scales(nc.sync, 1)
         load_w_words(1)
         load_bytes(3, 0, PACK)
-        load_bias_column(1)
+        bias_columns = load_value_bias_columns()
 
         def spread_bias(j):
             bank = psum.tile([P, PACK, P], F32, tag="acc", name="bias_bank", bufs=ACC_BANKS)
@@ -131,7 +129,6 @@ def tile_latent_cache_key_value_b2_kernel(
                 out=bias[:, j * F : (j + 1) * F].bitcast(F32).rearrange("p (n e) -> p n e", e=PACK),
                 in_=bank[:].rearrange("p e n -> p n e"),
             )
-
 
         wide, turned, grouped, c_codes, c_planes = {}, {}, {}, {}, {}
         sorted_slots = set()
@@ -190,8 +187,8 @@ def tile_latent_cache_key_value_b2_kernel(
 
         def quantize_cache(s0, count):
             width = PASSES * P
-            codes = keep.tile([P, count * width], U32, name="c_codes%d" % s0, align_bytes=256)
-            plane = keep.tile([P, count * width], U8, name="c_plane%d" % s0, align_bytes=256)
+            codes = keep.tile([P, count * width], U32, name="c_codes%d" % s0, align_bytes=OPERAND_ALIGN)
+            plane = keep.tile([P, count * width], U8, name="c_plane%d" % s0, align_bytes=OPERAND_ALIGN)
             nc.vector.quantize_mx(out=codes[:].bitcast(FP8X4), scales=plane[:], in_=grouped[s0][0][:])
             for i in range(count):
                 c_codes[s0 + i] = codes[:, i * width : (i + 1) * width]
@@ -245,7 +242,7 @@ def tile_latent_cache_key_value_b2_kernel(
             across[h] = flow.tile([P, PACK, P], F32, tag="across", name="across")
             for b in range(PACK):
                 nc.scalar.activation(
-                    out=across[h][:, b, :], in_=bank[:, b, :], func=IDENTITY, bias=bias_column[j][:, b, 0:1]
+                    out=across[h][:, b, :], in_=bank[:, b, :], func=IDENTITY, bias=bias_columns[:, b, 0:1]
                 )
 
         def turn_back(h, t):
@@ -280,21 +277,18 @@ def tile_latent_cache_key_value_b2_kernel(
                 in_=y_chunk[h, c][:, :, m0:m1].rearrange("p t (m i) -> p m t i", i=LINE),
             )
 
-        def round_on_gpsimd(h, c, m0, m1):
+        def round_half(h):
+            new_y_bf16(h, 0, "y_bf16_s", 2)
+            round_by_lines(nc.scalar.copy, h, 0, 0, N)
+            new_y_bf16(h, 1, "y_bf16_g", 1)
             nc.gpsimd.tensor_scalar(
-                out=y_bf16[h, c][:, PACK * m0 : PACK * m1].rearrange("p (m t) -> p m t", t=PACK),
-                in0=y_chunk[h, c][:, :, m0:m1].rearrange("p t m -> p m t"),
+                out=y_bf16[h, 1][:].rearrange("p (m t) -> p m t", t=PACK),
+                in0=y_chunk[h, 1].rearrange("p t m -> p m t"),
                 scalar1=1.0,
                 scalar2=0.0,
                 op0=MULT,
                 op1=ADD,
             )
-
-        def round_half(h):
-            new_y_bf16(h, 0, "y_bf16_s", 2)
-            round_by_lines(nc.scalar.copy, h, 0, 0, N)
-            new_y_bf16(h, 1, "y_bf16_g", 1)
-            round_on_gpsimd(h, 1, 0, GPSIMD_COLS)
 
         def quantize_y(h, c):
             g, j = divmod(h, 2)
@@ -312,6 +306,9 @@ def tile_latent_cache_key_value_b2_kernel(
                 out=y_words[g][:, j * F + N * c0 : j * F + N * c1], in_=y_codes[h][:, N * c0 : N * c1].bitcast(I32)
             )
 
+        def widen_slots_on_scalar(s0, s1):
+            widen_on_scalar(s0 * RUNS, s1 * RUNS)
+
         new_y_half(0)
         spread_bias(0)
         widen_on_vector(0)
@@ -325,11 +322,11 @@ def tile_latent_cache_key_value_b2_kernel(
         quantize_cache(1, 1)
         multiply(0, 0, 0)
         multiply(0, 0, 1)
-        widen_on_scalar(5 * RUNS, (5 + 1) * RUNS)
+        widen_slots_on_scalar(PACK + 1, PACK + 2)
         turn_slots(3, 1)
         quantize_cache(2, 1)
         add_bias(0, 0, 0)
-        widen_on_vector(4)
+        widen_on_vector(PACK)
         add_bias(0, 0, 1)
         store_slot(0, 0)
         multiply(0, 1, 0)
@@ -338,131 +335,46 @@ def tile_latent_cache_key_value_b2_kernel(
         quantize_cache(3, 1)
         add_bias(0, 1, 1)
         store_slot(0, 1)
-        widen_on_scalar(8 * RUNS, (8 + 1) * RUNS)
-        widen_on_scalar(9 * RUNS, (9 + 1) * RUNS)
-        multiply(0, 2, 0)
-        add_bias(0, 2, 0)
-        multiply(0, 2, 1)
-        add_bias(0, 2, 1)
-        store_slot(0, 2)
-        multiply(0, 3, 0)
-        add_bias(0, 3, 0)
-        multiply(0, 3, 1)
-        add_bias(0, 3, 1)
-        store_slot(0, 3)
+        widen_slots_on_scalar(2 * PACK, EARLY_SLOTS - 1)
+        for t in range(2, PACK):
+            for c in range(CHUNKS):
+                multiply(0, t, c)
+                add_bias(0, t, c)
+            store_slot(0, t)
         spread_bias(1)
         turn_slots(PACK, 2, "y_bf16_g", 1)
-        widen_on_scalar(10 * RUNS, (10 + 1) * RUNS)
-        widen_on_vector(6)
-        widen_on_vector(7)
+        widen_slots_on_scalar(EARLY_SLOTS - 1, EARLY_SLOTS)
+        widen_on_vector(PACK + 2)
+        widen_on_vector(PACK + 3)
         quantize_cache(PACK, 2)
 
-
-        def widened_after(step):
-            left = (SLOTS - 2 * PACK) * RUNS
-            return 2 * PACK * RUNS + (left * step + WIDEN_STEPS - 1) // WIDEN_STEPS
-
-        new_y_half(1)
-        multiply_across(1, 3)
-        round_half(0)
-        bank_pair(1, (0, 0), (0, 1))
-        store_slot(1, 0)
-        bank_pair(1, (1, 0), (1, 1))
-        store_slot(1, 1)
-        bank_pair(1, (2, 0), (2, 1))
-        store_slot(1, 2)
-        multiply(1, 3, 1)
-        add_bias(1, 3, 1)
-        quantize_y(0, 0)
-        turn_slots(6, 2)
-        turn_back(1, 3)
-        store_slot(1, 3)
-        quantize_cache(6, 2)
-        widen_on_scalar(88, 98)
-        quantize_y(0, 1)
-        store_codes(0, 0, CHUNKS)
-        new_y_half(2)
-        round_half(1)
-        bank_pair(2, (0, 0), (0, 1))
-        store_slot(2, 0)
-        bank_pair(2, (1, 0), (1, 1))
-        store_slot(2, 1)
-        bank_pair(2, (2, 0), (2, 1))
-        store_slot(2, 2)
-        bank_pair(2, (3, 0), (3, 1))
-        store_slot(2, 3)
-        quantize_y(1, 0)
-        turn_slots(8, 2)
-        quantize_cache(8, 2)
-        widen_on_scalar(98, 108)
-        quantize_y(1, 1)
-        store_codes(1, 0, CHUNKS)
-        new_y_half(3)
-        multiply_across(3, 3)
-        round_half(2)
-        bank_pair(3, (0, 0), (0, 1))
-        store_slot(3, 0)
-        bank_pair(3, (1, 0), (1, 1))
-        store_slot(3, 1)
-        bank_pair(3, (2, 0), (2, 1))
-        store_slot(3, 2)
-        multiply(3, 3, 1)
-        add_bias(3, 3, 1)
-        quantize_y(2, 0)
-        turn_slots(10, 2)
-        turn_back(3, 3)
-        store_slot(3, 3)
-        quantize_cache(10, 2)
-        widen_on_scalar(108, 118)
-        quantize_y(2, 1)
-        store_codes(2, 0, CHUNKS)
-        new_y_half(4)
-        round_half(3)
-        bank_pair(4, (0, 0), (0, 1))
-        store_slot(4, 0)
-        bank_pair(4, (1, 0), (1, 1))
-        store_slot(4, 1)
-        bank_pair(4, (2, 0), (2, 1))
-        store_slot(4, 2)
-        bank_pair(4, (3, 0), (3, 1))
-        store_slot(4, 3)
-        quantize_y(3, 0)
-        turn_slots(12, 2)
-        quantize_cache(12, 2)
-        widen_on_scalar(118, 128)
-        quantize_y(3, 1)
-        store_codes(3, 0, CHUNKS)
-        new_y_half(5)
-        multiply_across(5, 3)
-        round_half(4)
-        bank_pair(5, (0, 0), (0, 1))
-        store_slot(5, 0)
-        bank_pair(5, (1, 0), (1, 1))
-        store_slot(5, 1)
-        bank_pair(5, (2, 0), (2, 1))
-        store_slot(5, 2)
-        multiply(5, 3, 1)
-        add_bias(5, 3, 1)
-        quantize_y(4, 0)
-        turn_slots(14, 2)
-        turn_back(5, 3)
-        store_slot(5, 3)
-        quantize_cache(14, 2)
-        quantize_y(4, 1)
-        store_codes(4, 0, CHUNKS)
-        new_y_half(6)
-        round_half(5)
-        bank_pair(6, (0, 0), (0, 1))
-        store_slot(6, 0)
-        bank_pair(6, (1, 0), (1, 1))
-        store_slot(6, 1)
-        bank_pair(6, (2, 0), (2, 1))
-        store_slot(6, 2)
-        bank_pair(6, (3, 0), (3, 1))
-        store_slot(6, 3)
-        quantize_y(5, 0)
-        quantize_y(5, 1)
-        store_codes(5, 0, CHUNKS)
+        share = (SLOTS - EARLY_SLOTS) * RUNS // WIDEN_STEPS
+        last = PACK - 1
+        for h in range(1, HALVES - 1):
+            s = 2 * h + PACK
+            goes_across = h % 2 == 1
+            new_y_half(h)
+            if goes_across:
+                multiply_across(h, last)
+            round_half(h - 1)
+            for t in range(last if goes_across else PACK):
+                bank_pair(h, (t, 0), (t, 1))
+                store_slot(h, t)
+            if goes_across:
+                multiply(h, last, 1)
+                add_bias(h, last, 1)
+            quantize_y(h - 1, 0)
+            if s < SLOTS:
+                turn_slots(s, 2)
+            if goes_across:
+                turn_back(h, last)
+                store_slot(h, last)
+            if s < SLOTS:
+                quantize_cache(s, 2)
+            if h <= WIDEN_STEPS:
+                widen_on_scalar(EARLY_SLOTS * RUNS + share * (h - 1), EARLY_SLOTS * RUNS + share * h)
+            quantize_y(h - 1, 1)
+            store_codes(h - 1, 0, CHUNKS)
 
         h = HALVES - 1
         round_half(h - 1)

@@ -36,6 +36,14 @@ WIDEN_STEPS = 4
 OPERAND_ALIGN = 256
 LAST_SCALAR_COLS = 320
 
+ACROSS = (1, 3, 5)
+SINGLES = ()
+QC_LAST = ()
+SHARES = (0, 10, 10, 10, 10, 0, 0)
+BACK_FIRST = 0
+EXTRA = (0, 0, 0, 0, 0, 0, 0)
+BEFORE = (0, 0, 0, 0, 0, 0, 0)
+LATE_B1 = 0
 FLOPS = 2 * S * R * 2 * F
 
 
@@ -59,7 +67,9 @@ def tile_latent_cache_key_value_b2_kernel(
         bias = keep.tile([P, 2 * F], BF16, name="bias")
         w_words, w_scales, bias_words = [], [], []
         for j in range(2):
-            w_words.append(keep.tile([P, PASSES, 2 * F], U8, name="w_words%d" % j, align_bytes=OPERAND_ALIGN))
+            w_words.append(
+                keep.tile([P, PASSES, 2 * F], U8, name="w_words%d" % j, align_bytes=OPERAND_ALIGN)
+            )
             w_scales.append(keep.tile([P, PASSES, F], U8, name="w_scales%d" % j, align_bytes=OPERAND_ALIGN))
             bias_words.append(keep.tile([P, F // P], BF16, name="bias_words%d" % j))
             nc.vector.memset(w_scales[j][:].rearrange("p k n -> p (k n)").bitcast(I32), 0)
@@ -81,15 +91,16 @@ def tile_latent_cache_key_value_b2_kernel(
                 for t in range(PACK):
                     row_scale[PACK * g + t] = tile[:, g - g0, t * RUNS : (t + 1) * RUNS]
 
-        def load_w_words(j):
-            words = (k_words, v_words)[j]
+        def load_w_words(j, c0, c1):
+            cols = slice(2 * N * c0, 2 * N * c1)
+            words = (k_words, v_words)[j][:, :, cols]
             nc.sync.dma_start(
-                out=w_words[j][:].bitcast(I32), in_=words.rearrange("k p n -> p k n").bitcast(I32)
+                out=w_words[j][:, :, cols].bitcast(I32), in_=words.rearrange("k p n -> p k n").bitcast(I32)
             )
 
-        def load_w_scales(queue, j):
+        def load_w_scales(queue, j, q0=0, q1=QUADRANTS):
             scales = (k_scales, v_scales)[j]
-            for q in range(QUADRANTS):
+            for q in range(q0, q1):
                 queue.dma_start(
                     out=w_scales[j][32 * q : 32 * q + 4, :, :].bitcast(I32),
                     in_=scales[:, 4 * q : 4 * q + 4, :].rearrange("k r n -> r k n").bitcast(I32),
@@ -99,26 +110,30 @@ def tile_latent_cache_key_value_b2_kernel(
             row = (k_bias, v_bias)[j]
             nc.sync.dma_start(out=bias_words[j][:], in_=row.rearrange("o (p e) -> p (o e)", p=P))
 
-        def load_value_bias_columns():
-            tile = keep.tile([P, PACK, 2], BF16, name="bias_column1")
+        def load_bias_columns(j):
+            tile = keep.tile([P, PACK, 2], BF16, name="bias_column%d" % j)
             with nc.allow_non_contiguous_dma(reason="one bias value to a partition"):
-                nc.sync.dma_start(out=tile[:, :, 0:1], in_=v_bias[:, 0:N].rearrange("o (b p) -> p b o", p=P))
+                nc.sync.dma_start(out=tile[:, :, 0:1], in_=(k_bias, v_bias)[j][:, 0:N].rearrange("o (b p) -> p b o", p=P))
             return tile
 
-        load_bias(0)
         load_row_scales(0, 1)
         load_bytes(0, 0, 1)
+        load_bias(0)
+        load_bias(1)
         load_bytes(0, 1, PACK)
-        load_w_words(0)
-        load_w_scales(nc.scalar, 0)
+        load_w_words(0, 0, 1)
+        load_w_scales(nc.scalar, 0, 0, 2)
+        load_w_scales(nc.sync, 0, 2, 4)
+        load_w_words(0, 1, 2)
         load_bytes(1, 0, PACK)
         load_row_scales(1, GROUPS)
         load_bytes(2, 0, PACK)
-        load_bias(1)
+        if LATE_B1:
+            load_bias(1)
         load_w_scales(nc.sync, 1)
-        load_w_words(1)
+        load_w_words(1, 0, CHUNKS)
         load_bytes(3, 0, PACK)
-        bias_columns = load_value_bias_columns()
+        bias_columns = {j: load_bias_columns(j) for j in sorted({h % 2 for h in ACROSS}, reverse=True)}
 
         def spread_bias(j):
             bank = psum.tile([P, PACK, P], F32, tag="acc", name="bias_bank", bufs=ACC_BANKS)
@@ -133,11 +148,12 @@ def tile_latent_cache_key_value_b2_kernel(
         wide, turned, grouped, c_codes, c_planes = {}, {}, {}, {}, {}
         sorted_slots = set()
 
-        def widen_on_vector(s):
-            sorted_slots.add(s)
-            wide[s] = flow.tile([P, R], BF16, tag="wide", name="wide", bufs=WIDE_BUFS)
+        def widen_on_vector(s, b0=0, b1=RUNS):
+            if b0 == 0:
+                sorted_slots.add(s)
+                wide[s] = flow.tile([P, R], BF16, tag="wide", name="wide", bufs=WIDE_BUFS)
             sorted_view = wide[s][:].rearrange("p (k u q e) -> p k q u e", k=PASSES, u=2, e=2)
-            for b in range(RUNS):
+            for b in range(b0, b1):
                 k_pass, q0 = divmod(b * SCALED // PACK, P)
                 values = raw[s][:, b * SCALED : (b + 1) * SCALED].bitcast(FP8)
                 nc.vector.tensor_scalar(
@@ -185,6 +201,22 @@ def tile_latent_cache_key_value_b2_kernel(
             for i in range(count):
                 empty_turned(s0 + i)
 
+        def turn_first_slot(k_pass):
+            bank = psum.tile([P, 2, P], F32, tag="turn", name="turned")
+            words = wide[0][:].bitcast(F32)
+            for u in range(2):
+                word0 = 2 * P * k_pass + P * u
+                nc.tensor.transpose(bank[:, u, :], words[:, word0 : word0 + P], ident[:])
+            tile = keep.tile([P, PACK * P], BF16, name="first_grouped%d" % k_pass, align_bytes=64)
+            nc.scalar.copy(
+                out=tile[:].bitcast(F32).rearrange("p (r u) -> p r u", u=2), in_=bank[:].rearrange("p u r -> p r u")
+            )
+            return tile
+
+        def quantize_first_slot(k_pass, tile):
+            cols = slice(k_pass * P, (k_pass + 1) * P)
+            nc.vector.quantize_mx(out=c_codes[0][:, cols].bitcast(FP8X4), scales=c_planes[0][:, cols], in_=tile[:])
+
         def quantize_cache(s0, count):
             width = PASSES * P
             codes = keep.tile([P, count * width], U32, name="c_codes%d" % s0, align_bytes=OPERAND_ALIGN)
@@ -201,11 +233,12 @@ def tile_latent_cache_key_value_b2_kernel(
             for c in range(CHUNKS):
                 y_chunk[h, c] = y_half[h][:, :, N * c : N * (c + 1)]
 
-        def multiply(h, t, c):
+        def multiply(h, t, c, k0=0, k1=PASSES):
             g, j = divmod(h, 2)
             s = PACK * g + t
-            banks[h, t, c] = psum.tile([P, N], F32, tag="acc", name="acc", bufs=ACC_BANKS)
-            for k_pass in range(PASSES):
+            if k0 == 0:
+                banks[h, t, c] = psum.tile([P, N], F32, tag="acc", name="acc", bufs=ACC_BANKS)
+            for k_pass in range(k0, k1):
                 nc.tensor.matmul_mx(
                     out=banks[h, t, c][:],
                     lhsT=c_codes[s][:, k_pass * P : (k_pass + 1) * P].bitcast(FP8X4),
@@ -242,7 +275,7 @@ def tile_latent_cache_key_value_b2_kernel(
             across[h] = flow.tile([P, PACK, P], F32, tag="across", name="across")
             for b in range(PACK):
                 nc.scalar.activation(
-                    out=across[h][:, b, :], in_=bank[:, b, :], func=IDENTITY, bias=bias_columns[:, b, 0:1]
+                    out=across[h][:, b, :], in_=bank[:, b, :], func=IDENTITY, bias=bias_columns[j][:, b, 0:1]
                 )
 
         def turn_back(h, t):
@@ -277,18 +310,24 @@ def tile_latent_cache_key_value_b2_kernel(
                 in_=y_chunk[h, c][:, :, m0:m1].rearrange("p t (m i) -> p m t i", i=LINE),
             )
 
-        def round_half(h):
-            new_y_bf16(h, 0, "y_bf16_s", 2)
-            round_by_lines(nc.scalar.copy, h, 0, 0, N)
-            new_y_bf16(h, 1, "y_bf16_g", 1)
+        def round_on_gpsimd(h, c, m0):
             nc.gpsimd.tensor_scalar(
-                out=y_bf16[h, 1][:].rearrange("p (m t) -> p m t", t=PACK),
-                in0=y_chunk[h, 1].rearrange("p t m -> p m t"),
+                out=y_bf16[h, c][:, PACK * m0 :].rearrange("p (m t) -> p m t", t=PACK),
+                in0=y_chunk[h, c][:, :, m0:].rearrange("p t m -> p m t"),
                 scalar1=1.0,
                 scalar2=0.0,
                 op0=MULT,
                 op1=ADD,
             )
+
+        def round_half(h):
+            new_y_bf16(h, 0, "y_bf16_s", 2)
+            cols = N - EXTRA[h]
+            round_by_lines(nc.scalar.copy, h, 0, 0, cols)
+            new_y_bf16(h, 1, "y_bf16_g", 1)
+            round_on_gpsimd(h, 1, 0)
+            if cols < N:
+                round_on_gpsimd(h, 0, cols)
 
         def quantize_y(h, c):
             g, j = divmod(h, 2)
@@ -310,9 +349,10 @@ def tile_latent_cache_key_value_b2_kernel(
             widen_on_scalar(s0 * RUNS, s1 * RUNS)
 
         new_y_half(0)
-        spread_bias(0)
         widen_on_vector(0)
+        spread_bias(0)
         turn_slots(0, 1)
+        spread_bias(1)
         widen_on_vector(1)
         turn_slots(1, 1)
         widen_on_vector(2)
@@ -341,40 +381,53 @@ def tile_latent_cache_key_value_b2_kernel(
                 multiply(0, t, c)
                 add_bias(0, t, c)
             store_slot(0, t)
-        spread_bias(1)
         turn_slots(PACK, 2, "y_bf16_g", 1)
         widen_slots_on_scalar(EARLY_SLOTS - 1, EARLY_SLOTS)
         widen_on_vector(PACK + 2)
         widen_on_vector(PACK + 3)
         quantize_cache(PACK, 2)
 
-        share = (SLOTS - EARLY_SLOTS) * RUNS // WIDEN_STEPS
-        last = PACK - 1
+        widened = EARLY_SLOTS * RUNS
         for h in range(1, HALVES - 1):
             s = 2 * h + PACK
-            goes_across = h % 2 == 1
+            goes_across = h in ACROSS
+            order = (0, 2, 3, 1) if goes_across and h % 2 == 0 else (0, 1, 2, 3)
+            last = order[-1]
             new_y_half(h)
             if goes_across:
                 multiply_across(h, last)
+            widen_on_scalar(widened, widened + BEFORE[h])
+            widened = widened + BEFORE[h]
             round_half(h - 1)
-            for t in range(last if goes_across else PACK):
-                bank_pair(h, (t, 0), (t, 1))
+            for t in order[: 3 if goes_across else 4]:
+                if h in SINGLES:
+                    for c in range(CHUNKS):
+                        multiply(h, t, c)
+                        add_bias(h, t, c)
+                else:
+                    bank_pair(h, (t, 0), (t, 1))
                 store_slot(h, t)
             if goes_across:
                 multiply(h, last, 1)
                 add_bias(h, last, 1)
             quantize_y(h - 1, 0)
-            if s < SLOTS:
-                turn_slots(s, 2)
-            if goes_across:
+            if goes_across and BACK_FIRST:
                 turn_back(h, last)
                 store_slot(h, last)
             if s < SLOTS:
+                turn_slots(s, 2)
+            if goes_across and not BACK_FIRST:
+                turn_back(h, last)
+                store_slot(h, last)
+            if s < SLOTS and h not in QC_LAST:
                 quantize_cache(s, 2)
-            if h <= WIDEN_STEPS:
-                widen_on_scalar(EARLY_SLOTS * RUNS + share * (h - 1), EARLY_SLOTS * RUNS + share * h)
+            share = min(SHARES[h], SLOTS * RUNS - widened)
+            widen_on_scalar(widened, widened + share)
+            widened = widened + share
             quantize_y(h - 1, 1)
             store_codes(h - 1, 0, CHUNKS)
+            if s < SLOTS and h in QC_LAST:
+                quantize_cache(s, 2)
 
         h = HALVES - 1
         round_half(h - 1)

@@ -29,21 +29,13 @@ CHUNKS = F // N
 HALVES = 2 * GROUPS
 QUADRANTS = 4
 LINE = 4
-ACC_BANKS = 6
+BANKS = 8
 WIDE_BUFS = 8
 EARLY_SLOTS = 11
 WIDEN_STEPS = 4
 OPERAND_ALIGN = 256
 LAST_SCALAR_COLS = 320
 
-ACROSS = (1, 3, 5)
-SINGLES = ()
-QC_LAST = ()
-SHARES = (0, 10, 10, 10, 10, 0, 0)
-BACK_FIRST = 0
-EXTRA = (0, 0, 0, 0, 0, 0, 0)
-BEFORE = (0, 0, 0, 0, 0, 0, 0)
-LATE_B1 = 0
 FLOPS = 2 * S * R * 2 * F
 
 
@@ -60,16 +52,14 @@ def tile_latent_cache_key_value_b2_kernel(
     with ExitStack() as ctx:
         keep = ctx.enter_context(tc.tile_pool(name="keep", bufs=1))
         flow = ctx.enter_context(tc.tile_pool(name="flow", bufs=2))
-        psum = ctx.enter_context(tc.psum_pool(name="psum", bufs=2))
+        psum = ctx.enter_context(tc.psum_pool(name="psum", bufs=BANKS))
         ctx.enter_context(tc.manual_schedule())
 
         ident = keep.tile([P, P], F32, name="ident")
         bias = keep.tile([P, 2 * F], BF16, name="bias")
         w_words, w_scales, bias_words = [], [], []
         for j in range(2):
-            w_words.append(
-                keep.tile([P, PASSES, 2 * F], U8, name="w_words%d" % j, align_bytes=OPERAND_ALIGN)
-            )
+            w_words.append(keep.tile([P, PASSES, 2 * F], U8, name="w_words%d" % j, align_bytes=OPERAND_ALIGN))
             w_scales.append(keep.tile([P, PASSES, F], U8, name="w_scales%d" % j, align_bytes=OPERAND_ALIGN))
             bias_words.append(keep.tile([P, F // P], BF16, name="bias_words%d" % j))
             nc.vector.memset(w_scales[j][:].rearrange("p k n -> p (k n)").bitcast(I32), 0)
@@ -98,7 +88,7 @@ def tile_latent_cache_key_value_b2_kernel(
                 out=w_words[j][:, :, cols].bitcast(I32), in_=words.rearrange("k p n -> p k n").bitcast(I32)
             )
 
-        def load_w_scales(queue, j, q0=0, q1=QUADRANTS):
+        def load_w_scales(queue, j, q0, q1):
             scales = (k_scales, v_scales)[j]
             for q in range(q0, q1):
                 queue.dma_start(
@@ -110,10 +100,10 @@ def tile_latent_cache_key_value_b2_kernel(
             row = (k_bias, v_bias)[j]
             nc.sync.dma_start(out=bias_words[j][:], in_=row.rearrange("o (p e) -> p (o e)", p=P))
 
-        def load_bias_columns(j):
-            tile = keep.tile([P, PACK, 2], BF16, name="bias_column%d" % j)
+        def load_value_bias_columns():
+            tile = keep.tile([P, PACK, 2], BF16, name="bias_columns")
             with nc.allow_non_contiguous_dma(reason="one bias value to a partition"):
-                nc.sync.dma_start(out=tile[:, :, 0:1], in_=(k_bias, v_bias)[j][:, 0:N].rearrange("o (b p) -> p b o", p=P))
+                nc.sync.dma_start(out=tile[:, :, 0:1], in_=v_bias[:, 0:N].rearrange("o (b p) -> p b o", p=P))
             return tile
 
         load_row_scales(0, 1)
@@ -122,21 +112,19 @@ def tile_latent_cache_key_value_b2_kernel(
         load_bias(1)
         load_bytes(0, 1, PACK)
         load_w_words(0, 0, 1)
-        load_w_scales(nc.scalar, 0, 0, 2)
-        load_w_scales(nc.sync, 0, 2, 4)
-        load_w_words(0, 1, 2)
+        load_w_scales(nc.scalar, 0, 0, QUADRANTS // 2)
+        load_w_scales(nc.sync, 0, QUADRANTS // 2, QUADRANTS)
+        load_w_words(0, 1, CHUNKS)
         load_bytes(1, 0, PACK)
         load_row_scales(1, GROUPS)
         load_bytes(2, 0, PACK)
-        if LATE_B1:
-            load_bias(1)
-        load_w_scales(nc.sync, 1)
+        load_w_scales(nc.sync, 1, 0, QUADRANTS)
         load_w_words(1, 0, CHUNKS)
         load_bytes(3, 0, PACK)
-        bias_columns = {j: load_bias_columns(j) for j in sorted({h % 2 for h in ACROSS}, reverse=True)}
+        bias_columns = load_value_bias_columns()
 
         def spread_bias(j):
-            bank = psum.tile([P, PACK, P], F32, tag="acc", name="bias_bank", bufs=ACC_BANKS)
+            bank = psum.tile([P, PACK, P], F32, tag="bank", name="bias_bank")
             words = bias_words[j][:].bitcast(F32)
             for e in range(PACK):
                 nc.tensor.transpose(bank[:, e, :], words[:, e : e + 1].to_broadcast([P, P]), ident[:])
@@ -148,12 +136,11 @@ def tile_latent_cache_key_value_b2_kernel(
         wide, turned, grouped, c_codes, c_planes = {}, {}, {}, {}, {}
         sorted_slots = set()
 
-        def widen_on_vector(s, b0=0, b1=RUNS):
-            if b0 == 0:
-                sorted_slots.add(s)
-                wide[s] = flow.tile([P, R], BF16, tag="wide", name="wide", bufs=WIDE_BUFS)
+        def widen_on_vector(s):
+            sorted_slots.add(s)
+            wide[s] = flow.tile([P, R], BF16, tag="wide", name="wide", bufs=WIDE_BUFS)
             sorted_view = wide[s][:].rearrange("p (k u q e) -> p k q u e", k=PASSES, u=2, e=2)
-            for b in range(b0, b1):
+            for b in range(RUNS):
                 k_pass, q0 = divmod(b * SCALED // PACK, P)
                 values = raw[s][:, b * SCALED : (b + 1) * SCALED].bitcast(FP8)
                 nc.vector.tensor_scalar(
@@ -175,7 +162,7 @@ def tile_latent_cache_key_value_b2_kernel(
                 )
 
         def turn(s):
-            turned[s] = psum.tile([P, PASSES, 2, P], F32, tag="turn", name="turned")
+            turned[s] = psum.tile([P, PASSES, 2, P], F32, tag="bank", name="turned")
             words = wide[s][:].bitcast(F32)
             for k_pass in range(PASSES):
                 word0 = 2 * P * k_pass
@@ -193,29 +180,19 @@ def tile_latent_cache_key_value_b2_kernel(
                 in_=turned[s][:].rearrange("p k u r -> p k r u"),
             )
 
-        def turn_slots(s0, count, tag="grouped", bufs=3):
-            tile = flow.tile([P, count * R], BF16, tag=tag, name="grouped", bufs=bufs, align_bytes=64)
+        def handed_on(h):
+            tag = "handed_on%d" % (min(h, HALVES - 3) % 2)
+            return flow.tile([P, N * PACK], BF16, tag=tag, name="handed_on", bufs=1, align_bytes=64)
+
+        def turn_slots(s0, count, tile):
             for i in range(count):
                 grouped[s0 + i] = (tile, i)
                 turn(s0 + i)
             for i in range(count):
                 empty_turned(s0 + i)
 
-        def turn_first_slot(k_pass):
-            bank = psum.tile([P, 2, P], F32, tag="turn", name="turned")
-            words = wide[0][:].bitcast(F32)
-            for u in range(2):
-                word0 = 2 * P * k_pass + P * u
-                nc.tensor.transpose(bank[:, u, :], words[:, word0 : word0 + P], ident[:])
-            tile = keep.tile([P, PACK * P], BF16, name="first_grouped%d" % k_pass, align_bytes=64)
-            nc.scalar.copy(
-                out=tile[:].bitcast(F32).rearrange("p (r u) -> p r u", u=2), in_=bank[:].rearrange("p u r -> p r u")
-            )
-            return tile
-
-        def quantize_first_slot(k_pass, tile):
-            cols = slice(k_pass * P, (k_pass + 1) * P)
-            nc.vector.quantize_mx(out=c_codes[0][:, cols].bitcast(FP8X4), scales=c_planes[0][:, cols], in_=tile[:])
+        def turn_single(s):
+            turn_slots(s, 1, flow.tile([P, R], BF16, tag="single", name="single", bufs=3, align_bytes=64))
 
         def quantize_cache(s0, count):
             width = PASSES * P
@@ -233,12 +210,11 @@ def tile_latent_cache_key_value_b2_kernel(
             for c in range(CHUNKS):
                 y_chunk[h, c] = y_half[h][:, :, N * c : N * (c + 1)]
 
-        def multiply(h, t, c, k0=0, k1=PASSES):
+        def multiply(h, t, c):
             g, j = divmod(h, 2)
             s = PACK * g + t
-            if k0 == 0:
-                banks[h, t, c] = psum.tile([P, N], F32, tag="acc", name="acc", bufs=ACC_BANKS)
-            for k_pass in range(k0, k1):
+            banks[h, t, c] = psum.tile([P, N], F32, tag="bank", name="acc")
+            for k_pass in range(PASSES):
                 nc.tensor.matmul_mx(
                     out=banks[h, t, c][:],
                     lhsT=c_codes[s][:, k_pass * P : (k_pass + 1) * P].bitcast(FP8X4),
@@ -260,7 +236,7 @@ def tile_latent_cache_key_value_b2_kernel(
         def multiply_across(h, t):
             g, j = divmod(h, 2)
             s = PACK * g + t
-            bank = psum.tile([P, PACK, P], F32, tag="acc", name="acc_across", bufs=ACC_BANKS)
+            bank = psum.tile([P, PACK, P], F32, tag="bank", name="acc_across")
             for b in range(PACK):
                 for k_pass in range(PASSES):
                     nc.tensor.matmul_mx(
@@ -275,11 +251,11 @@ def tile_latent_cache_key_value_b2_kernel(
             across[h] = flow.tile([P, PACK, P], F32, tag="across", name="across")
             for b in range(PACK):
                 nc.scalar.activation(
-                    out=across[h][:, b, :], in_=bank[:, b, :], func=IDENTITY, bias=bias_columns[j][:, b, 0:1]
+                    out=across[h][:, b, :], in_=bank[:, b, :], func=IDENTITY, bias=bias_columns[:, b, 0:1]
                 )
 
         def turn_back(h, t):
-            bank = psum.tile([P, PACK, P], F32, tag="acc", name="turned_back", bufs=ACC_BANKS)
+            bank = psum.tile([P, PACK, P], F32, tag="bank", name="turned_back")
             for b in range(PACK):
                 nc.tensor.transpose(bank[:, b, :], across[h][:, b, :], ident[:])
             nc.scalar.copy(out=y_chunk[h, 0][:, t, :], in_=bank[:].rearrange("p b n -> p (b n)"))
@@ -310,24 +286,18 @@ def tile_latent_cache_key_value_b2_kernel(
                 in_=y_chunk[h, c][:, :, m0:m1].rearrange("p t (m i) -> p m t i", i=LINE),
             )
 
-        def round_on_gpsimd(h, c, m0):
+        def round_half(h):
+            new_y_bf16(h, 0, "y_bf16_s", 2)
+            round_by_lines(nc.scalar.copy, h, 0, 0, N)
+            y_bf16[h, 1] = handed_on(h)
             nc.gpsimd.tensor_scalar(
-                out=y_bf16[h, c][:, PACK * m0 :].rearrange("p (m t) -> p m t", t=PACK),
-                in0=y_chunk[h, c][:, :, m0:].rearrange("p t m -> p m t"),
+                out=y_bf16[h, 1][:].rearrange("p (m t) -> p m t", t=PACK),
+                in0=y_chunk[h, 1].rearrange("p t m -> p m t"),
                 scalar1=1.0,
                 scalar2=0.0,
                 op0=MULT,
                 op1=ADD,
             )
-
-        def round_half(h):
-            new_y_bf16(h, 0, "y_bf16_s", 2)
-            cols = N - EXTRA[h]
-            round_by_lines(nc.scalar.copy, h, 0, 0, cols)
-            new_y_bf16(h, 1, "y_bf16_g", 1)
-            round_on_gpsimd(h, 1, 0)
-            if cols < N:
-                round_on_gpsimd(h, 0, cols)
 
         def quantize_y(h, c):
             g, j = divmod(h, 2)
@@ -351,19 +321,19 @@ def tile_latent_cache_key_value_b2_kernel(
         new_y_half(0)
         widen_on_vector(0)
         spread_bias(0)
-        turn_slots(0, 1)
+        turn_single(0)
         spread_bias(1)
         widen_on_vector(1)
-        turn_slots(1, 1)
+        turn_single(1)
         widen_on_vector(2)
         quantize_cache(0, 1)
-        turn_slots(2, 1)
+        turn_single(2)
         widen_on_vector(3)
         quantize_cache(1, 1)
         multiply(0, 0, 0)
         multiply(0, 0, 1)
         widen_slots_on_scalar(PACK + 1, PACK + 2)
-        turn_slots(3, 1)
+        turn_single(3)
         quantize_cache(2, 1)
         add_bias(0, 0, 0)
         widen_on_vector(PACK)
@@ -381,53 +351,41 @@ def tile_latent_cache_key_value_b2_kernel(
                 multiply(0, t, c)
                 add_bias(0, t, c)
             store_slot(0, t)
-        turn_slots(PACK, 2, "y_bf16_g", 1)
+        turn_slots(PACK, 2, handed_on(0))
         widen_slots_on_scalar(EARLY_SLOTS - 1, EARLY_SLOTS)
         widen_on_vector(PACK + 2)
         widen_on_vector(PACK + 3)
         quantize_cache(PACK, 2)
 
-        widened = EARLY_SLOTS * RUNS
+        share = (SLOTS - EARLY_SLOTS) * RUNS // WIDEN_STEPS
+        last = PACK - 1
         for h in range(1, HALVES - 1):
             s = 2 * h + PACK
-            goes_across = h in ACROSS
-            order = (0, 2, 3, 1) if goes_across and h % 2 == 0 else (0, 1, 2, 3)
-            last = order[-1]
+            goes_across = h % 2 == 1
             new_y_half(h)
+            bank_pair(h, (0, 0), (0, 1))
+            store_slot(h, 0)
             if goes_across:
                 multiply_across(h, last)
-            widen_on_scalar(widened, widened + BEFORE[h])
-            widened = widened + BEFORE[h]
             round_half(h - 1)
-            for t in order[: 3 if goes_across else 4]:
-                if h in SINGLES:
-                    for c in range(CHUNKS):
-                        multiply(h, t, c)
-                        add_bias(h, t, c)
-                else:
-                    bank_pair(h, (t, 0), (t, 1))
+            for t in range(1, last if goes_across else PACK):
+                bank_pair(h, (t, 0), (t, 1))
                 store_slot(h, t)
             if goes_across:
                 multiply(h, last, 1)
                 add_bias(h, last, 1)
-            quantize_y(h - 1, 0)
-            if goes_across and BACK_FIRST:
-                turn_back(h, last)
-                store_slot(h, last)
             if s < SLOTS:
-                turn_slots(s, 2)
-            if goes_across and not BACK_FIRST:
+                turn_slots(s, 2, handed_on(h))
+            if goes_across:
                 turn_back(h, last)
                 store_slot(h, last)
-            if s < SLOTS and h not in QC_LAST:
+            if h <= WIDEN_STEPS:
+                widen_on_scalar(EARLY_SLOTS * RUNS + share * (h - 1), EARLY_SLOTS * RUNS + share * h)
+            quantize_y(h - 1, 0)
+            if s < SLOTS:
                 quantize_cache(s, 2)
-            share = min(SHARES[h], SLOTS * RUNS - widened)
-            widen_on_scalar(widened, widened + share)
-            widened = widened + share
             quantize_y(h - 1, 1)
             store_codes(h - 1, 0, CHUNKS)
-            if s < SLOTS and h in QC_LAST:
-                quantize_cache(s, 2)
 
         h = HALVES - 1
         round_half(h - 1)

@@ -31,7 +31,7 @@ QUADRANTS = 4
 LINE = 4
 BANKS = 8
 WIDE_BUFS = 8
-EARLY_SLOTS = 11
+EARLY_SLOTS = 10
 WIDEN_STEPS = 4
 OPERAND_ALIGN = 256
 LAST_SCALAR_COLS = 320
@@ -345,7 +345,7 @@ def tile_latent_cache_key_value_b2_kernel(
         quantize_cache(3, 1)
         add_bias(0, 1, 1)
         store_slot(0, 1)
-        widen_slots_on_scalar(2 * PACK, EARLY_SLOTS - 1)
+        widen_slots_on_scalar(PACK + 3, EARLY_SLOTS - 1)
         for t in range(2, PACK):
             for c in range(CHUNKS):
                 multiply(0, t, c)
@@ -354,7 +354,6 @@ def tile_latent_cache_key_value_b2_kernel(
         turn_slots(PACK, 2, handed_on(0))
         widen_slots_on_scalar(EARLY_SLOTS - 1, EARLY_SLOTS)
         widen_on_vector(PACK + 2)
-        widen_on_vector(PACK + 3)
         quantize_cache(PACK, 2)
 
         share = (SLOTS - EARLY_SLOTS) * RUNS // WIDEN_STEPS

@@ -210,20 +210,22 @@ def tile_latent_cache_key_value_b2_kernel(
             for c in range(CHUNKS):
                 y_chunk[h, c] = y_half[h][:, :, N * c : N * (c + 1)]
 
-        def multiply(h, t, c):
+        def multiply(h, *named):
             g, j = divmod(h, 2)
-            s = PACK * g + t
-            banks[h, t, c] = psum.tile([P, N], F32, tag="bank", name="acc")
+            for t, c in named:
+                banks[h, t, c] = psum.tile([P, N], F32, tag="bank", name="acc")
             for k_pass in range(PASSES):
-                nc.tensor.matmul_mx(
-                    out=banks[h, t, c][:],
-                    lhsT=c_codes[s][:, k_pass * P : (k_pass + 1) * P].bitcast(FP8X4),
-                    lhsT_scale=c_planes[s][:, k_pass * P : (k_pass + 1) * P],
-                    rhs=w_words[j][:, k_pass, 2 * N * c : 2 * N * (c + 1)].bitcast(FP4X4),
-                    rhs_scale=w_scales[j][:, k_pass, N * c : N * (c + 1)],
-                    start=(k_pass == 0),
-                    stop=(k_pass == PASSES - 1),
-                )
+                for t, c in named:
+                    s = PACK * g + t
+                    nc.tensor.matmul_mx(
+                        out=banks[h, t, c][:],
+                        lhsT=c_codes[s][:, k_pass * P : (k_pass + 1) * P].bitcast(FP8X4),
+                        lhsT_scale=c_planes[s][:, k_pass * P : (k_pass + 1) * P],
+                        rhs=w_words[j][:, k_pass, 2 * N * c : 2 * N * (c + 1)].bitcast(FP4X4),
+                        rhs_scale=w_scales[j][:, k_pass, N * c : N * (c + 1)],
+                        start=(k_pass == 0),
+                        stop=(k_pass == PASSES - 1),
+                    )
 
         def add_bias(h, t, c):
             col0 = (h % 2) * F + N * c
@@ -261,8 +263,7 @@ def tile_latent_cache_key_value_b2_kernel(
             nc.scalar.copy(out=y_chunk[h, 0][:, t, :], in_=bank[:].rearrange("p b n -> p (b n)"))
 
         def bank_pair(h, earlier, later):
-            multiply(h, *earlier)
-            multiply(h, *later)
+            multiply(h, earlier, later)
             add_bias(h, *later)
             add_bias(h, *earlier)
 
@@ -330,8 +331,8 @@ def tile_latent_cache_key_value_b2_kernel(
         turn_single(2)
         widen_on_vector(3)
         quantize_cache(1, 1)
-        multiply(0, 0, 0)
-        multiply(0, 0, 1)
+        multiply(0, (0, 0))
+        multiply(0, (0, 1))
         widen_slots_on_scalar(PACK + 1, PACK + 2)
         turn_single(3)
         quantize_cache(2, 1)
@@ -339,8 +340,8 @@ def tile_latent_cache_key_value_b2_kernel(
         widen_on_vector(PACK)
         add_bias(0, 0, 1)
         store_slot(0, 0)
-        multiply(0, 1, 0)
-        multiply(0, 1, 1)
+        multiply(0, (1, 0))
+        multiply(0, (1, 1))
         add_bias(0, 1, 0)
         quantize_cache(3, 1)
         add_bias(0, 1, 1)
@@ -348,7 +349,7 @@ def tile_latent_cache_key_value_b2_kernel(
         widen_slots_on_scalar(PACK + 3, EARLY_SLOTS - 1)
         for t in range(2, PACK):
             for c in range(CHUNKS):
-                multiply(0, t, c)
+                multiply(0, (t, c))
                 add_bias(0, t, c)
             store_slot(0, t)
         turn_slots(PACK, 2, handed_on(0))
@@ -371,7 +372,7 @@ def tile_latent_cache_key_value_b2_kernel(
                 bank_pair(h, (t, 0), (t, 1))
                 store_slot(h, t)
             if goes_across:
-                multiply(h, last, 1)
+                multiply(h, (last, 1))
                 add_bias(h, last, 1)
             if s < SLOTS:
                 turn_slots(s, 2, handed_on(h))

from contextlib import ExitStack

import concourse.mybir as mybir
from concourse.masks import make_identity

F32 = mybir.dt.float32
BF16 = mybir.dt.bfloat16
I32 = mybir.dt.int32
U32 = mybir.dt.uint32
U8 = mybir.dt.uint8
FP8 = mybir.dt.float8_e4m3fn
FP8X4 = mybir.dt.float8_e4m3fn_x4
FP4X4 = mybir.dt.float4_e2m1fn_x4
ADD = mybir.AluOpType.add
MULT = mybir.AluOpType.mult
COPY = mybir.ActivationFunctionType.Copy
IDENTITY = mybir.ActivationFunctionType.Identity

S, R, F = 2048, 1024, 1024
P = 128
PACK = 4
GROUPS = S // (P * PACK)
SLOTS = GROUPS * PACK
PASSES = R // (P * PACK)
SCALED = 128
RUNS = R // SCALED
N = 512
CHUNKS = F // N
HALVES = 2 * GROUPS
QUADRANTS = 4
LINE = 4
BANKS = 8
WIDE_BUFS = 8
EARLY_SLOTS = 10
WIDEN_STEPS = 4
OPERAND_ALIGN = 256
LAST_SCALAR_COLS = 320

FLOPS = 2 * S * R * 2 * F


def tile_latent_cache_key_value_b2_kernel(
    tc, C_bytes, C_scale, k_words, k_scales, v_words, v_scales, k_bias, v_bias, out_0, out_1, out_2
):
    nc = tc.nc
    c_rows = C_bytes.rearrange("(g p t) r -> g p (t r)", p=P, t=PACK)
    c_scale_rows = C_scale.rearrange("(g p t) b -> p g (t b)", p=P, t=PACK)
    y_rows = out_0.rearrange("(g p t) j h d -> g j p t (h d)", p=P, t=PACK)
    y_words = out_1.rearrange("g p m t -> g p (m t)").bitcast(I32)
    y_scales = out_2.bitcast(I32)

    with ExitStack() as ctx:
        keep = ctx.enter_context(tc.tile_pool(name="keep", bufs=1))
        flow = ctx.enter_context(tc.tile_pool(name="flow", bufs=2))
        psum = ctx.enter_context(tc.psum_pool(name="psum", bufs=BANKS))
        ctx.enter_context(tc.manual_schedule())

        ident = keep.tile([P, P], F32, name="ident")
        bias = keep.tile([P, 2 * F], BF16, name="bias")
        w_words, w_scales, bias_words = [], [], []
        for j in range(2):
            w_words.append(keep.tile([P, PASSES, 2 * F], U8, name="w_words%d" % j, align_bytes=OPERAND_ALIGN))
            w_scales.append(keep.tile([P, PASSES, F], U8, name="w_scales%d" % j, align_bytes=OPERAND_ALIGN))
            bias_words.append(keep.tile([P, F // P], BF16, name="bias_words%d" % j))
            nc.vector.memset(w_scales[j][:].rearrange("p k n -> p (k n)").bitcast(I32), 0)
        nc.vector.memset(ident[:], 0.0)
        make_identity(nc, ident[:], nomemset=True)

        raw, row_scale = {}, {}

        def load_bytes(g, t0, t1):
            tile = keep.tile([P, (t1 - t0) * R], U8, name="raw%d_%d" % (g, t0))
            nc.sync.dma_start(out=tile[:], in_=c_rows[g][:, t0 * R : t1 * R])
            for t in range(t0, t1):
                raw[PACK * g + t] = tile[:, (t - t0) * R : (t - t0 + 1) * R]

        def load_row_scales(g0, g1):
            tile = keep.tile([P, g1 - g0, PACK * RUNS], F32, name="row_scale%d" % g0)
            nc.sync.dma_start(out=tile[:], in_=c_scale_rows[:, g0:g1, :])
            for g in range(g0, g1):
                for t in range(PACK):
                    row_scale[PACK * g + t] = tile[:, g - g0, t * RUNS : (t + 1) * RUNS]

        def load_w_words(j, c0, c1):
            cols = slice(2 * N * c0, 2 * N * c1)
            words = (k_words, v_words)[j][:, :, cols]
            nc.sync.dma_start(
                out=w_words[j][:, :, cols].bitcast(I32), in_=words.rearrange("k p n -> p k n").bitcast(I32)
            )

        def load_w_scales(queue, j, q0, q1):
            scales = (k_scales, v_scales)[j]
            for q in range(q0, q1):
                queue.dma_start(
                    out=w_scales[j][32 * q : 32 * q + 4, :, :].bitcast(I32),
                    in_=scales[:, 4 * q : 4 * q + 4, :].rearrange("k r n -> r k n").bitcast(I32),
                )

        def load_bias(j):
            row = (k_bias, v_bias)[j]
            nc.sync.dma_start(out=bias_words[j][:], in_=row.rearrange("o (p e) -> p (o e)", p=P))

        def load_value_bias_columns():
            tile = keep.tile([P, PACK, 2], BF16, name="bias_columns")
            with nc.allow_non_contiguous_dma(reason="one bias value to a partition"):
                nc.sync.dma_start(out=tile[:, :, 0:1], in_=v_bias[:, 0:N].rearrange("o (b p) -> p b o", p=P))
            return tile

        load_row_scales(0, 1)
        load_bytes(0, 0, 1)
        load_bias(0)
        load_bias(1)
        load_bytes(0, 1, PACK)
        load_w_words(0, 0, 1)
        load_w_scales(nc.scalar, 0, 0, QUADRANTS // 2)
        load_w_scales(nc.sync, 0, QUADRANTS // 2, QUADRANTS)
        load_w_words(0, 1, CHUNKS)
        load_bytes(1, 0, PACK)
        load_row_scales(1, GROUPS)
        load_bytes(2, 0, PACK)
        load_w_scales(nc.sync, 1, 0, QUADRANTS)
        load_w_words(1, 0, CHUNKS)
        load_bytes(3, 0, PACK)
        bias_columns = load_value_bias_columns()

        def spread_bias(j):
            bank = psum.tile([P, PACK, P], F32, tag="bank", name="bias_bank")
            words = bias_words[j][:].bitcast(F32)
            for e in range(PACK):
                nc.tensor.transpose(bank[:, e, :], words[:, e : e + 1].to_broadcast([P, P]), ident[:])
            nc.scalar.copy(
                out=bias[:, j * F : (j + 1) * F].bitcast(F32).rearrange("p (n e) -> p n e", e=PACK),
                in_=bank[:].rearrange("p e n -> p n e"),
            )

        wide, turned, grouped, c_codes, c_planes = {}, {}, {}, {}, {}
        sorted_slots = set()

        def widen_on_vector(s):
            sorted_slots.add(s)
            wide[s] = flow.tile([P, R], BF16, tag="wide", name="wide", bufs=WIDE_BUFS)
            sorted_view = wide[s][:].rearrange("p (k u q e) -> p k q u e", k=PASSES, u=2, e=2)
            for b in range(RUNS):
                k_pass, q0 = divmod(b * SCALED // PACK, P)
                values = raw[s][:, b * SCALED : (b + 1) * SCALED].bitcast(FP8)
                nc.vector.tensor_scalar(
                    out=sorted_view[:, k_pass, q0 : q0 + SCALED // PACK, :, :],
                    in0=values.rearrange("p (q u e) -> p q u e", u=2, e=2),
                    scalar1=row_scale[s][:, b : b + 1],
                    scalar2=None,
                    op0=MULT,
                )

        def widen_on_scalar(first, last):
            for n in range(first, last):
                s, b = divmod(n, RUNS)
                if b == 0:
                    wide[s] = flow.tile([P, R], BF16, tag="wide", name="wide", bufs=WIDE_BUFS)
                cols = slice(b * SCALED, (b + 1) * SCALED)
                nc.scalar.activation(
                    out=wide[s][:, cols], in_=raw[s][:, cols].bitcast(FP8), func=COPY, scale=row_scale[s][:, b : b + 1]
                )

        def turn(s):
            turned[s] = psum.tile([P, PASSES, 2, P], F32, tag="bank", name="turned")
            words = wide[s][:].bitcast(F32)
            for k_pass in range(PASSES):
                word0 = 2 * P * k_pass
                for u in range(2):
                    if s in sorted_slots:
                        src = words[:, word0 + P * u : word0 + P * (u + 1)]
                    else:
                        src = words[:, word0 + u : word0 + 2 * P : 2]
                    nc.tensor.transpose(turned[s][:, k_pass, u, :], src, ident[:])

        def empty_turned(s):
            tile, i = grouped[s]
            nc.scalar.copy(
                out=tile[:, i * R : (i + 1) * R].bitcast(F32).rearrange("p (k r u) -> p k r u", k=PASSES, u=2),
                in_=turned[s][:].rearrange("p k u r -> p k r u"),
            )

        def handed_on(h):
            tag = "handed_on%d" % (min(h, HALVES - 3) % 2)
            return flow.tile([P, N * PACK], BF16, tag=tag, name="handed_on", bufs=1, align_bytes=64)

        def turn_slots(s0, count, tile):
            for i in range(count):
                grouped[s0 + i] = (tile, i)
                turn(s0 + i)
            for i in range(count):
                empty_turned(s0 + i)

        def turn_single(s):
            turn_slots(s, 1, flow.tile([P, R], BF16, tag="single", name="single", bufs=3, align_bytes=64))

        def quantize_cache(s0, count):
            width = PASSES * P
            codes = keep.tile([P, count * width], U32, name="c_codes%d" % s0, align_bytes=OPERAND_ALIGN)
            plane = keep.tile([P, count * width], U8, name="c_plane%d" % s0, align_bytes=OPERAND_ALIGN)
            nc.vector.quantize_mx(out=codes[:].bitcast(FP8X4), scales=plane[:], in_=grouped[s0][0][:])
            for i in range(count):
                c_codes[s0 + i] = codes[:, i * width : (i + 1) * width]
                c_planes[s0 + i] = plane[:, i * width : (i + 1) * width]

        banks, y_half, y_chunk = {}, {}, {}

        def new_y_half(h):
            y_half[h] = flow.tile([P, PACK, F], F32, tag="y_f32", name="y_f32", bufs=5)
            for c in range(CHUNKS):
                y_chunk[h, c] = y_half[h][:, :, N * c : N * (c + 1)]

        def multiply(h, *named):
            g, j = divmod(h, 2)
            for t, c in named:
                banks[h, t, c] = psum.tile([P, N], F32, tag="bank", name="acc")
            for k_pass in range(PASSES):
                for t, c in named:
                    s = PACK * g + t
                    nc.tensor.matmul_mx(
                        out=banks[h, t, c][:],
                        lhsT=c_codes[s][:, k_pass * P : (k_pass + 1) * P].bitcast(FP8X4),
                        lhsT_scale=c_planes[s][:, k_pass * P : (k_pass + 1) * P],
                        rhs=w_words[j][:, k_pass, 2 * N * c : 2 * N * (c + 1)].bitcast(FP4X4),
                        rhs_scale=w_scales[j][:, k_pass, N * c : N * (c + 1)],
                        start=(k_pass == 0),
                        stop=(k_pass == PASSES - 1),
                    )

        def add_bias(h, t, c):
            col0 = (h % 2) * F + N * c
            nc.vector.tensor_tensor(
                out=y_chunk[h, c][:, t, :], in0=banks[h, t, c][:], in1=bias[:, col0 : col0 + N], op=ADD
            )

        across = {}

        def multiply_across(h, t):
            g, j = divmod(h, 2)
            s = PACK * g + t
            bank = psum.tile([P, PACK, P], F32, tag="bank", name="acc_across")
            for b in range(PACK):
                for k_pass in range(PASSES):
                    nc.tensor.matmul_mx(
                        out=bank[:, b, :],
                        lhsT=w_words[j][:, k_pass, 2 * P * b : 2 * P * (b + 1)].bitcast(FP4X4),
                        lhsT_scale=w_scales[j][:, k_pass, P * b : P * (b + 1)],
                        rhs=c_codes[s][:, k_pass * P : (k_pass + 1) * P].bitcast(FP8X4),
                        rhs_scale=c_planes[s][:, k_pass * P : (k_pass + 1) * P],
                        start=(k_pass == 0),
                        stop=(k_pass == PASSES - 1),
                    )
            across[h] = flow.tile([P, PACK, P], F32, tag="across", name="across")
            for b in range(PACK):
                nc.scalar.activation(
                    out=across[h][:, b, :], in_=bank[:, b, :], func=IDENTITY, bias=bias_columns[:, b, 0:1]
                )

        def turn_back(h, t):
            bank = psum.tile([P, PACK, P], F32, tag="bank", name="turned_back")
            for b in range(PACK):
                nc.tensor.transpose(bank[:, b, :], across[h][:, b, :], ident[:])
            nc.scalar.copy(out=y_chunk[h, 0][:, t, :], in_=bank[:].rearrange("p b n -> p (b n)"))

        def bank_pair(h, earlier, later):
            multiply(h, earlier, later)
            add_bias(h, *later)
            add_bias(h, *earlier)

        def store_slot(h, t):
            g, j = divmod(h, 2)
            nc.sync.dma_start(out=y_rows[g][j][:, t : t + 1, :], in_=y_half[h][:, t : t + 1, :])

        def store_chunk(h, c, t0, t1):
            g, j = divmod(h, 2)
            nc.sync.dma_start(out=y_rows[g][j][:, t0:t1, N * c : N * (c + 1)], in_=y_chunk[h, c][:, t0:t1, :])

        y_bf16, y_codes = {}, {}
        y_plane = keep.tile([P, 2 * F], U8, name="y_plane", align_bytes=64)

        def new_y_bf16(h, c, tag, bufs):
            y_bf16[h, c] = flow.tile([P, N * PACK], BF16, tag=tag, name=tag, bufs=bufs, align_bytes=64)

        def round_by_lines(copy, h, c, m0, m1):
            copy(
                out=y_bf16[h, c][:, PACK * m0 : PACK * m1].rearrange("p (m i t) -> p m t i", i=LINE, t=PACK),
                in_=y_chunk[h, c][:, :, m0:m1].rearrange("p t (m i) -> p m t i", i=LINE),
            )

        def round_half(h):
            new_y_bf16(h, 0, "y_bf16_s", 2)
            round_by_lines(nc.scalar.copy, h, 0, 0, N)
            y_bf16[h, 1] = handed_on(h)
            nc.gpsimd.tensor_scalar(
                out=y_bf16[h, 1][:].rearrange("p (m t) -> p m t", t=PACK),
                in0=y_chunk[h, 1].rearrange("p t m -> p m t"),
                scalar1=1.0,
                scalar2=0.0,
                op0=MULT,
                op1=ADD,
            )

        def quantize_y(h, c):
            g, j = divmod(h, 2)
            if c == 0:
                y_codes[h] = flow.tile([P, F], U32, tag="y_codes", name="y_codes", bufs=HALVES, align_bytes=64)
            nc.vector.quantize_mx(
                out=y_codes[h][:, N * c : N * (c + 1)].bitcast(FP8X4),
                scales=y_plane[4 * g :, j * F + N * c : j * F + N * (c + 1)],
                in_=y_bf16[h, c][:],
            )

        def store_codes(h, c0, c1):
            g, j = divmod(h, 2)
            nc.sync.dma_start(
                out=y_words[g][:, j * F + N * c0 : j * F + N * c1], in_=y_codes[h][:, N * c0 : N * c1].bitcast(I32)
            )

        def widen_slots_on_scalar(s0, s1):
            widen_on_scalar(s0 * RUNS, s1 * RUNS)

        new_y_half(0)
        widen_on_vector(0)
        spread_bias(0)
        turn_single(0)
        spread_bias(1)
        widen_on_vector(1)
        turn_single(1)
        widen_on_vector(2)
        quantize_cache(0, 1)
        turn_single(2)
        widen_on_vector(3)
        quantize_cache(1, 1)
        multiply(0, (0, 0))
        multiply(0, (0, 1))
        widen_slots_on_scalar(PACK + 1, PACK + 2)
        turn_single(3)
        quantize_cache(2, 1)
        add_bias(0, 0, 0)
        widen_on_vector(PACK)
        add_bias(0, 0, 1)
        store_slot(0, 0)
        multiply(0, (1, 0))
        multiply(0, (1, 1))
        add_bias(0, 1, 0)
        quantize_cache(3, 1)
        add_bias(0, 1, 1)
        store_slot(0, 1)
        widen_slots_on_scalar(PACK + 3, EARLY_SLOTS - 1)
        for t in range(2, PACK):
            for c in range(CHUNKS):
                multiply(0, (t, c))
                add_bias(0, t, c)
            store_slot(0, t)
        turn_slots(PACK, 2, handed_on(0))
        widen_slots_on_scalar(EARLY_SLOTS - 1, EARLY_SLOTS)
        widen_on_vector(PACK + 2)
        quantize_cache(PACK, 2)

        share = (SLOTS - EARLY_SLOTS) * RUNS // WIDEN_STEPS
        last = PACK - 1
        for h in range(1, HALVES - 1):
            s = 2 * h + PACK
            goes_across = h % 2 == 1
            new_y_half(h)
            bank_pair(h, (0, 0), (0, 1))
            store_slot(h, 0)
            if goes_across:
                multiply_across(h, last)
            round_half(h - 1)
            for t in range(1, last if goes_across else PACK):
                bank_pair(h, (t, 0), (t, 1))
                store_slot(h, t)
            if goes_across:
                multiply(h, (last, 1))
                add_bias(h, last, 1)
            if s < SLOTS:
                turn_slots(s, 2, handed_on(h))
            if goes_across:
                turn_back(h, last)
                store_slot(h, last)
            if h <= WIDEN_STEPS:
                widen_on_scalar(EARLY_SLOTS * RUNS + share * (h - 1), EARLY_SLOTS * RUNS + share * h)
            quantize_y(h - 1, 0)
            if s < SLOTS:
                quantize_cache(s, 2)
            quantize_y(h - 1, 1)
            store_codes(h - 1, 0, CHUNKS)

        h = HALVES - 1
        round_half(h - 1)
        for c in range(CHUNKS):
            tile = keep.tile([P, PACK, N], F32, name="y_last%d" % c)
            y_chunk[h, c] = tile[:]
            for t in range(0, PACK, 2):
                bank_pair(h, (t, c), (t + 1, c))
                store_chunk(h, c, t, t + 2)
            if c == 0:
                new_y_bf16(h, 0, "y_bf16_s", 2)
                round_by_lines(nc.scalar.copy, h, 0, 0, N)
        for c in range(CHUNKS):
            quantize_y(h - 1, c)
        store_codes(h - 1, 0, CHUNKS)
        new_y_bf16(h, 1, "y_bf16_last", 1)
        round_by_lines(nc.scalar.copy, h, 1, 0, LAST_SCALAR_COLS)
        round_by_lines(nc.vector.tensor_copy, h, 1, LAST_SCALAR_COLS, N)
        for c in range(CHUNKS):
            quantize_y(h, c)
            store_codes(h, c, c + 1)
        for q in range(QUADRANTS):
            nc.scalar.dma_start(
                out=y_scales[:, 4 * q : 4 * q + 4, :], in_=y_plane[32 * q : 32 * q + 4 * GROUPS, :].bitcast(I32)
            )
